import numpy as np
import ml_dtypes


def mxq(x, axis, fmt="e4m3"):
    dtype, down = {"e4m3": (ml_dtypes.float8_e4m3fn, 7), "e5m2": (ml_dtypes.float8_e5m2, 14)}[fmt]
    v = np.moveaxis(np.asarray(x, np.float32).astype(ml_dtypes.bfloat16).astype(np.float64), axis, -1)
    blocks = v.reshape(v.shape[:-1] + (-1, 32))
    amax = np.abs(blocks).max(-1, keepdims=True)
    byte = np.maximum(np.where(amax > 0, np.frexp(amax)[1] - 1 + 127, 0) - down, 1)
    scale = np.exp2(byte - 127.0)
    codes = (blocks / scale).astype(np.float32).astype(dtype).astype(np.float64)
    return np.moveaxis((codes * scale).reshape(v.shape), -1, axis)


WIDE = False


def mx_kscale(k):
    if not WIDE:
        return np.ones(k)
    levels = np.array([10, -10, 5, -5, 0])
    if k % 512:
        return np.exp2(np.random.permutation(np.resize(levels, k // 32))).repeat(32)
    a = np.empty((k // 512, 16))
    for p in range(k // 512):
        a[p, :8] = np.random.permutation(np.resize(levels, 8))
        for g in range(8):
            far = levels[np.abs(levels - a[p, g]) >= 10]
            a[p, g + 8] = far[np.random.randint(len(far))]
    return np.exp2(a.ravel()).repeat(32)


def f64(x):
    return np.asarray(x).astype(np.float64)


def striped(idx):
    return np.tile(idx.reshape(-1, 16).T, (8, 1)).astype(np.uint16)


def unstriped(offs):
    return offs[:16].T.reshape(-1).astype(np.int64)


def pack_weight(w):
    k, n = w.shape
    w = f64(np.asarray(w, np.float32).astype(ml_dtypes.bfloat16)).reshape(k // 32, 32, n)
    amax = np.abs(w).max(1)
    byte = np.clip(np.where(amax > 0, np.frexp(amax)[1] - 1 + 127 - 7, 1), 1, 254)
    scaled = (w * np.exp2(127.0 - byte)[:, None, :]).reshape(k, n).astype(np.float32)
    words = np.ascontiguousarray(scaled.reshape(k // 512, 128, 4, n).transpose(0, 1, 3, 2)).astype(ml_dtypes.float8_e4m3fn).view(np.uint8)
    return words, np.ascontiguousarray(byte.astype(np.uint8).reshape(k // 512, 16, n))


def unpack_weight(words, scales):
    g, p, n, _ = words.shape
    vals = np.ascontiguousarray(words).view(ml_dtypes.float8_e4m3fn).astype(np.float64) * np.repeat(np.exp2(scales.astype(np.float64) - 127.0), 8, axis=1)[..., None]
    return vals.transpose(0, 1, 3, 2).reshape(g * 512, n)


def gelu(v):
    return 0.5 * v * (1.0 + np.tanh(np.sqrt(2.0 / np.pi) * (v + 0.044715 * v**3)))


K, T, D, H, N = 1024, 512, 3, 512, 256
P = 2 ** 7


def setup_inputs():
    n = np.random.standard_normal
    s = mx_kscale(K)[:, None]
    u = mx_kscale(H)
    packed_xT = pack_weight(n((K, T)) * s)
    return {
        "x_words": packed_xT[0],
        "x_scales": packed_xT[1],
        "w1": (n((K, H)) / np.sqrt(K) / s * u).astype(np.float32),
        "w2": (n((H, N)) / np.sqrt(H) / u[:, None]).astype(np.float32),
        "gate": (np.tile(np.random.uniform(0.2, 1.0, (D, 1, T)) / np.sqrt(D), (1, P, 1))).astype(np.float32),
        "pos1": striped(np.random.permutation(T)),
        "pos2": striped(np.random.permutation(T)),
        "pos3": striped(np.random.permutation(T)),
    }


def reference(x_words, x_scales, w1, w2, gate, pos1, pos2, pos3):
    xq = unpack_weight(x_words, x_scales)
    h = gelu(mxq(f64(w1), 0, "e4m3").T @ xq)
    z = h - (h[:, unstriped(pos1)] * f64(gate)[0, :1] + h[:, unstriped(pos2)] * f64(gate)[1, :1] + h[:, unstriped(pos3)] * f64(gate)[2, :1])
    return mxq(f64(w2), 0, "e4m3").T @ mxq(z, 0, "e4m3")

@@ -1,0 +1,292 @@
+from contextlib import ExitStack
+
+import concourse.mybir as mybir
+from concourse.masks import make_identity
+
+K, T, D, H, N = 1024, 512, 3, 512, 256
+FLOPS = 2 * K * H * T + 2 * H * N * T
+
+F32 = mybir.dt.float32
+BF16 = mybir.dt.bfloat16
+I32 = mybir.dt.int32
+U32 = mybir.dt.uint32
+U16 = mybir.dt.uint16
+U8 = mybir.dt.uint8
+FP8X4 = mybir.dt.float8_e4m3fn_x4
+GELU = mybir.ActivationFunctionType.Gelu_apprx_tanh
+COPY = mybir.ActivationFunctionType.Copy
+MULT = mybir.AluOpType.mult
+
+P = 128
+PACK = 4
+PASSES = K // (P * PACK)
+H_TILES = H // P
+V_BLOCKS = T // P
+M_TILES = N // P
+SPARE = 16
+ALIGN = 64
+OVERLAP = 16
+STRIP = H_TILES * T + T
+STEPS = [(0, 0, 4), (1, 0, 4), (2, 0, 2), (3, 0, 2), (2, 2, 3), (3, 2, 3), (2, 3, 4), (3, 3, 4)]
+
+
+def interleave_views(grouped, raw):
+    return (
+        grouped.rearrange("p (c i) j -> p c j i", i=4),
+        raw.rearrange("p j (c i) -> p c j i", i=4),
+    )
+
+
+def tile_picked_wlapl_gelu_l_kernel(
+    tc, x_words, x_scales, w1, w2, gate, pos1, pos2, pos3, out
+):
+    nc = tc.nc
+    with ExitStack() as ctx:
+        lists = ctx.enter_context(tc.tile_pool(name="lists", bufs=1))
+        keep = ctx.enter_context(tc.tile_pool(name="keep", bufs=1))
+        sums = ctx.enter_context(tc.psum_pool(name="sums", bufs=1))
+        work = ctx.enter_context(tc.psum_pool(name="work", bufs=4))
+
+        def sb(shape, dtype, name, tag=""):
+            return keep.tile(shape, dtype, name=name, tag=tag or name, align_bytes=ALIGN)
+
+        x_plane = sb([P, T], U8, "x_plane")
+        nc.vector.memset(x_plane[:].bitcast(U32), 0)
+        zeros = sb([P, SPARE], F32, "zeros")
+        nc.vector.memset(zeros[:], 0.0)
+        for q in range(4):
+            nc.scalar.dma_start(
+                out=x_plane[32 * q : 32 * q + 4 * PASSES, :].bitcast(I32),
+                in_=x_scales[:, 4 * q : 4 * q + 4, :].bitcast(I32),
+            )
+        h = [sb([P, T + SPARE], F32, f"h{t}") for t in range(H_TILES)]
+        nc.scalar.activation(out=h[0][:, T:], in_=zeros[:], func=GELU)
+        ident = sb([P, P], F32, "ident")
+        make_identity(nc, ident[:])
+        for t in range(1, H_TILES):
+            nc.gpsimd.memset(h[t][:, T:], 0.0)
+
+        w1_rows = w1.rearrange("(z p j) c -> z p j c", z=PASSES, j=PACK)
+        w1_raw = {}
+
+        def load_w1(t0, t1):
+            for z in range(PASSES):
+                raw = sb([P, PACK, (t1 - t0) * P], F32, f"w1_raw{t0}_{z}")
+                nc.sync.dma_start(out=raw[:], in_=w1_rows[z, :, :, t0 * P : t1 * P])
+                for t in range(t0, t1):
+                    w1_raw[t, z] = raw[:, :, (t - t0) * P : (t - t0 + 1) * P]
+
+        gate_raw = [sb([P, T], F32, f"gate_raw{d}") for d in range(D)]
+        minus_gate = [sb([P, T], F32, f"minus_gate{d}") for d in range(D)]
+        offsets = [lists.tile([P, T // 16], U16, name=f"offsets{d}") for d in range(D)]
+        pos = [pos1, pos2, pos3]
+
+        def load_neighbour(d):
+            nc.sync.dma_start(out=gate_raw[d][:], in_=gate[d])
+            nc.sync.dma_start(offsets[d][:], pos[d])
+
+        load_w1(0, 1)
+        x_codes = [sb([P, T], U32, f"x_codes{z}") for z in range(PASSES)]
+        for z in range(PASSES):
+            nc.sync.dma_start(
+                out=x_codes[z][:].bitcast(I32),
+                in_=x_words[z].rearrange("p n r -> p (n r)").bitcast(I32),
+            )
+        load_neighbour(0)
+        load_neighbour(1)
+        load_w1(1, 2)
+        load_neighbour(2)
+        load_w1(2, 4)
+        w2_raw = sb([P, PACK, N], F32, "w2_raw")
+        nc.sync.dma_start(out=w2_raw[:], in_=w2.rearrange("(p j) n -> p j n", j=PACK))
+
+        strips = [sb([P, STRIP], F32, f"strip{d}") for d in range(D)]
+        head = {}
+        top = STRIP
+        for t, b0, b1 in STEPS:
+            head[t, b0] = top - (b1 - b0) * P
+            top = head[t, b0] + OVERLAP
+
+        def room_before(t, d, b0, words):
+            end = head[t, b0] + OVERLAP
+            return strips[d][:, end - words : end]
+
+        def hidden(t, codes, scales):
+            acc = work.tile([P, T], F32, name=f"h_acc{t}", tag="work")
+            for z in range(PASSES):
+                nc.tensor.matmul_mx(
+                    out=acc[:],
+                    lhsT=codes[z].bitcast(FP8X4),
+                    lhsT_scale=scales[z],
+                    rhs=x_codes[z][:].bitcast(FP8X4),
+                    rhs_scale=x_plane[4 * z :, :],
+                    start=(z == 0),
+                    stop=(z == PASSES - 1),
+                )
+            nc.scalar.activation(out=h[t][:, :T], in_=acc[:], func=GELU)
+
+        def first_hidden():
+            codes, scales, grouped = [], [], []
+            for z in range(PASSES):
+                g = sb([P, P, PACK], BF16, f"w1_grouped0_{z}")
+                dst, src = interleave_views(g[:], w1_raw[0, z])
+                nc.vector.tensor_copy(out=dst, in_=src)
+                grouped.append(g)
+            for z in range(PASSES):
+                c = sb([P, P], U32, f"w1_codes0_{z}")
+                s = sb([P, P], U8, f"w1_scales0_{z}")
+                nc.vector.quantize_mx(
+                    out=c[:].bitcast(FP8X4), scales=s[:], in_=grouped[z][:].rearrange("p c j -> p (c j)")
+                )
+                codes.append(c[:])
+                scales.append(s[:])
+            hidden(0, codes, scales)
+
+        def later_hidden(t, flat):
+            g = flat.rearrange("p (z c j) -> p z c j", z=PASSES, j=PACK)
+            for z in range(PASSES):
+                dst, src = interleave_views(g[:, z], w1_raw[t, z])
+                nc.scalar.copy(out=dst, in_=src)
+            c = sb([P, PASSES * P], U32, f"w1_codes{t}")
+            s = sb([P, PASSES * P], U8, f"w1_scales{t}")
+            nc.vector.quantize_mx(
+                out=c[:].bitcast(FP8X4), scales=s[:], in_=flat
+            )
+            hidden(
+                t,
+                [c[:, z * P : (z + 1) * P] for z in range(PASSES)],
+                [s[:, z * P : (z + 1) * P] for z in range(PASSES)],
+            )
+
+        z_t = [sums.tile([P, H], F32, name=f"z_t{b}") for b in range(V_BLOCKS)]
+
+        def add_turned(t, b, values, start, stop):
+            nc.tensor.matmul(
+                out=z_t[b][:, t * P : (t + 1) * P],
+                lhsT=values,
+                rhs=ident[:],
+                is_transpose=True,
+                start=start,
+                stop=stop,
+            )
+
+        def neighbour(t, d, b0, b1, place=None):
+            if d == 0:
+                for b in range(b0, b1):
+                    add_turned(t, b, h[t][:, b * P : (b + 1) * P], True, False)
+            width = (b1 - b0) * P
+            term = strips[d][:, head[t, b0] : head[t, b0] + width] if place is None else place
+            nc.vector.tensor_tensor(
+                term,
+                h[t][:].indirect(offsets[d][:, b0 * P // 16 : b1 * P // 16]),
+                minus_gate[d][:, b0 * P : b1 * P],
+                MULT,
+            )
+            for b in range(b0, b1):
+                add_turned(t, b, term[:, (b - b0) * P : (b - b0 + 1) * P], False, d == D - 1)
+
+        last_room = sb([P, 3 * P - OVERLAP], F32, "last_room")
+        z_words = [
+            room_before(3, 2, 2, 2 * P),
+            sb([P, 2 * P], F32, "z_words1")[:],
+            last_room[:, : 2 * P],
+            sb([P, 2 * P], F32, "z_words3")[:],
+        ]
+        z_rows = [w.bitcast(BF16).rearrange("v (u p e) -> v u p e", u=2, e=2) for w in z_words]
+        z_grouped = [
+            room_before(2, 0, 3, 2 * P),
+            room_before(2, 1, 3, 2 * P),
+            sb([P, 2 * P], F32, "z_grouped2")[:],
+            sb([P, 2 * P], F32, "z_grouped3")[:],
+        ]
+
+        def round_z(b, t0, t1, on_vector=False):
+            src = z_t[b][:].rearrange("v (p u e) -> v u p e", u=2, e=2)[:, :, 32 * t0 : 32 * t1, :]
+            dst = z_rows[b][:, :, 32 * t0 : 32 * t1, :]
+            if on_vector:
+                nc.vector.tensor_copy(out=dst, in_=src)
+            else:
+                nc.scalar.copy(out=dst, in_=src)
+
+        out_rows = out.rearrange("(a m) v -> m a v", a=M_TILES)
+
+        def turn_back(b):
+            words = z_words[b]
+            back = work.tile([P, 2, P], F32, name=f"back{b}", tag="work")
+            for u in range(2):
+                nc.tensor.transpose(back[:, u, :], words[:, u * P : (u + 1) * P], ident[:])
+            nc.scalar.copy(out=z_grouped[b].rearrange("p (v u) -> p v u", u=2), in_=back[:].rearrange("p u v -> p v u"))
+
+        def second_layer(b, w2_codes, w2_scales, out_on_vector=False):
+            grouped = z_grouped[b].bitcast(BF16)
+            codes = sb([P, P], U32, f"z_codes{b}")
+            scales = sb([P, P], U8, f"z_scales{b}")
+            nc.vector.quantize_mx(
+                out=codes[:].bitcast(FP8X4), scales=scales[:], in_=grouped
+            )
+            acc = work.tile([P, M_TILES, P], F32, name=f"out_acc{b}", tag="work")
+            for a in range(M_TILES):
+                nc.tensor.matmul_mx(
+                    out=acc[:, a, :],
+                    lhsT=w2_codes[:, a * P : (a + 1) * P].bitcast(FP8X4),
+                    lhsT_scale=w2_scales[:, a * P : (a + 1) * P],
+                    rhs=codes[:].bitcast(FP8X4),
+                    rhs_scale=scales[:],
+                    start=True,
+                    stop=True,
+                )
+            result = sb([P, M_TILES, P], F32, f"result{b}")
+            if out_on_vector:
+                nc.vector.tensor_copy(out=result[:], in_=acc[:])
+            else:
+                nc.scalar.copy(out=result[:], in_=acc[:])
+            nc.sync.dma_start(out=out_rows[:, :, b * P : (b + 1) * P], in_=result[:])
+
+        first_hidden()
+        for d in range(2):
+            nc.vector.tensor_scalar_mul(minus_gate[d][:], gate_raw[d][:], -1.0)
+        neighbour(0, 0, 0, 4)
+        neighbour(0, 1, 0, 4)
+        later_hidden(1, room_before(0, 2, 0, T).bitcast(BF16))
+        nc.scalar.activation(out=minus_gate[2][:], in_=gate_raw[2][:], func=COPY, scale=-1.0)
+        neighbour(0, 2, 0, 4)
+        neighbour(1, 0, 0, 4)
+        later_hidden(2, room_before(1, 1, 0, T).bitcast(BF16))
+        neighbour(1, 1, 0, 4)
+        later_hidden(3, room_before(1, 2, 0, T).bitcast(BF16))
+        neighbour(1, 2, 0, 4)
+
+        w2_grouped = room_before(2, 1, 0, T).bitcast(BF16)
+        dst, src = interleave_views(w2_grouped.rearrange("p (n j) -> p n j", j=PACK), w2_raw[:])
+        nc.scalar.copy(out=dst, in_=src)
+        for b in range(V_BLOCKS):
+            round_z(b, 0, 2)
+        neighbour(2, 0, 0, 2)
+        w2_codes = sb([P, N], U32, "w2_codes")
+        w2_scales = sb([P, N], U8, "w2_scales")
+        nc.vector.quantize_mx(out=w2_codes[:].bitcast(FP8X4), scales=w2_scales[:], in_=w2_grouped)
+        neighbour(2, 1, 0, 2)
+        neighbour(2, 2, 0, 2)
+        for d in range(D):
+            neighbour(3, d, 0, 2)
+        round_z(0, 2, 4)
+        round_z(1, 2, 4)
+        turn_back(0)
+        turn_back(1)
+        for d in range(D):
+            neighbour(2, d, 2, 3)
+        for d in range(D):
+            neighbour(3, d, 2, 3)
+        round_z(2, 2, 4)
+        second_layer(0, w2_codes, w2_scales)
+        second_layer(1, w2_codes, w2_scales)
+        turn_back(2)
+        for d in range(D):
+            neighbour(2, d, 3, 4)
+        neighbour(3, 0, 3, 4)
+        neighbour(3, 1, 3, 4, last_room[:, 2 * P - OVERLAP :])
+        neighbour(3, 2, 3, 4)
+        second_layer(2, w2_codes, w2_scales, out_on_vector=True)
+        round_z(3, 2, 4, on_vector=True)
+        turn_back(3)
+        second_layer(3, w2_codes, w2_scales)

@@ -50,15 +50,19 @@ def tile_picked_wlapl_gelu_l_kernel(
         def sb(shape, dtype, name, tag=""):
             return keep.tile(shape, dtype, name=name, tag=tag or name, align_bytes=ALIGN)
 
-        x_plane = sb([P, T], U8, "x_plane")
-        nc.vector.memset(x_plane[:].bitcast(U32), 0)
-        zeros = sb([P, SPARE], F32, "zeros")
-        nc.vector.memset(zeros[:], 0.0)
+        x_rows = sb([P, T // 4], I32, "x_rows")
         for q in range(4):
             nc.scalar.dma_start(
-                out=x_plane[32 * q : 32 * q + 4 * PASSES, :].bitcast(I32),
+                out=x_rows[32 * q : 32 * q + 4 * PASSES, :],
                 in_=x_scales[:, 4 * q : 4 * q + 4, :].bitcast(I32),
             )
+        zeros = sb([P, SPARE], F32, "zeros")
+        nc.vector.memset(zeros[:], 0.0)
+        x_plane = sb([P, T], U8, "x_plane")
+        nc.vector.memset(x_plane[:].bitcast(I32), 0)
+        for q in range(4):
+            rows = slice(32 * q, 32 * q + 4 * PASSES)
+            nc.vector.tensor_copy(out=x_plane[rows, :].bitcast(I32), in_=x_rows[rows, :])
         h = [sb([P, T + SPARE], F32, f"h{t}") for t in range(H_TILES)]
         nc.scalar.activation(out=h[0][:, T:], in_=zeros[:], func=GELU)
         ident = sb([P, P], F32, "ident")
@@ -111,19 +115,23 @@ def tile_picked_wlapl_gelu_l_kernel(
             end = head[t, b0] + OVERLAP
             return strips[d][:, end - words : end]
 
-        def hidden(t, codes, scales):
-            acc = work.tile([P, T], F32, name=f"h_acc{t}", tag="work")
+        def hidden(t, codes, scales, pieces=1):
+            width = T // pieces
+            accs = [work.tile([P, width], F32, name=f"h_acc{t}_{i}", tag="work") for i in range(pieces)]
             for z in range(PASSES):
-                nc.tensor.matmul_mx(
-                    out=acc[:],
-                    lhsT=codes[z].bitcast(FP8X4),
-                    lhsT_scale=scales[z],
-                    rhs=x_codes[z][:].bitcast(FP8X4),
-                    rhs_scale=x_plane[4 * z :, :],
-                    start=(z == 0),
-                    stop=(z == PASSES - 1),
-                )
-            nc.scalar.activation(out=h[t][:, :T], in_=acc[:], func=GELU)
+                for i in range(pieces):
+                    cols = slice(i * width, (i + 1) * width)
+                    nc.tensor.matmul_mx(
+                        out=accs[i][:],
+                        lhsT=codes[z].bitcast(FP8X4),
+                        lhsT_scale=scales[z],
+                        rhs=x_codes[z][:, cols].bitcast(FP8X4),
+                        rhs_scale=x_plane[4 * z :, cols],
+                        start=(z == 0),
+                        stop=(z == PASSES - 1),
+                    )
+            for i in range(pieces):
+                nc.scalar.activation(out=h[t][:, i * width : (i + 1) * width], in_=accs[i][:], func=GELU)
 
         def first_hidden():
             codes, scales, grouped = [], [], []
@@ -140,7 +148,7 @@ def tile_picked_wlapl_gelu_l_kernel(
                 )
                 codes.append(c[:])
                 scales.append(s[:])
-            hidden(0, codes, scales)
+            hidden(0, codes, scales, pieces=2)
 
         def later_hidden(t, flat):
             g = flat.rearrange("p (z c j) -> p z c j", z=PASSES, j=PACK)
@@ -160,9 +168,12 @@ def tile_picked_wlapl_gelu_l_kernel(
 
         z_t = [sums.tile([P, H], F32, name=f"z_t{b}") for b in range(V_BLOCKS)]
 
+        def bank_of(t, b):
+            return z_t[0] if (t, b) == (H_TILES - 1, V_BLOCKS - 1) else z_t[b]
+
         def add_turned(t, b, values, start, stop):
             nc.tensor.matmul(
-                out=z_t[b][:, t * P : (t + 1) * P],
+                out=bank_of(t, b)[:, t * P : (t + 1) * P],
                 lhsT=values,
                 rhs=ident[:],
                 is_transpose=True,
@@ -185,23 +196,12 @@ def tile_picked_wlapl_gelu_l_kernel(
             for b in range(b0, b1):
                 add_turned(t, b, term[:, (b - b0) * P : (b - b0 + 1) * P], False, d == D - 1)
 
-        last_room = sb([P, 3 * P - OVERLAP], F32, "last_room")
-        z_words = [
-            room_before(3, 2, 2, 2 * P),
-            sb([P, 2 * P], F32, "z_words1")[:],
-            last_room[:, : 2 * P],
-            sb([P, 2 * P], F32, "z_words3")[:],
-        ]
+        z_words = [sb([P, 2 * P], F32, f"z_words{b}")[:] for b in range(V_BLOCKS)]
         z_rows = [w.bitcast(BF16).rearrange("v (u p e) -> v u p e", u=2, e=2) for w in z_words]
-        z_grouped = [
-            room_before(2, 0, 3, 2 * P),
-            room_before(2, 1, 3, 2 * P),
-            sb([P, 2 * P], F32, "z_grouped2")[:],
-            sb([P, 2 * P], F32, "z_grouped3")[:],
-        ]
+        z_grouped = [sb([P, 2 * P], F32, f"z_grouped{b}")[:] for b in range(V_BLOCKS)]
 
         def round_z(b, t0, t1, on_vector=False):
-            src = z_t[b][:].rearrange("v (p u e) -> v u p e", u=2, e=2)[:, :, 32 * t0 : 32 * t1, :]
+            src = bank_of(t0, b)[:].rearrange("v (p u e) -> v u p e", u=2, e=2)[:, :, 32 * t0 : 32 * t1, :]
             dst = z_rows[b][:, :, 32 * t0 : 32 * t1, :]
             if on_vector:
                 nc.vector.tensor_copy(out=dst, in_=src)
@@ -217,7 +217,7 @@ def tile_picked_wlapl_gelu_l_kernel(
                 nc.tensor.transpose(back[:, u, :], words[:, u * P : (u + 1) * P], ident[:])
             nc.scalar.copy(out=z_grouped[b].rearrange("p (v u) -> p v u", u=2), in_=back[:].rearrange("p u v -> p v u"))
 
-        def second_layer(b, w2_codes, w2_scales, out_on_vector=False):
+        def second_layer(b, w2_codes, w2_scales, out_on_vector=False, split=False):
             grouped = z_grouped[b].bitcast(BF16)
             codes = sb([P, P], U32, f"z_codes{b}")
             scales = sb([P, P], U8, f"z_scales{b}")
@@ -225,9 +225,10 @@ def tile_picked_wlapl_gelu_l_kernel(
                 out=codes[:].bitcast(FP8X4), scales=scales[:], in_=grouped
             )
             acc = work.tile([P, M_TILES, P], F32, name=f"out_acc{b}", tag="work")
+            places = [acc[:, 0, :], z_t[1][:, :P] if split else acc[:, 1, :]]
             for a in range(M_TILES):
                 nc.tensor.matmul_mx(
-                    out=acc[:, a, :],
+                    out=places[a],
                     lhsT=w2_codes[:, a * P : (a + 1) * P].bitcast(FP8X4),
                     lhsT_scale=w2_scales[:, a * P : (a + 1) * P],
                     rhs=codes[:].bitcast(FP8X4),
@@ -235,6 +236,14 @@ def tile_picked_wlapl_gelu_l_kernel(
                     start=True,
                     stop=True,
                 )
+            if split:
+                low = sb([P, P], F32, "result_low")
+                high = sb([P, P], F32, "result_high")
+                nc.vector.tensor_copy(out=low[:], in_=places[0])
+                nc.sync.dma_start(out=out_rows[:, 0, b * P : (b + 1) * P], in_=low[:])
+                nc.scalar.copy(out=high[:], in_=places[1])
+                nc.scalar.dma_start(out=out_rows[:, 1, b * P : (b + 1) * P], in_=high[:])
+                return
             result = sb([P, M_TILES, P], F32, f"result{b}")
             if out_on_vector:
                 nc.vector.tensor_copy(out=result[:], in_=acc[:])
@@ -283,10 +292,11 @@ def tile_picked_wlapl_gelu_l_kernel(
         turn_back(2)
         for d in range(D):
             neighbour(2, d, 3, 4)
+        round_z(3, 2, 3)
         neighbour(3, 0, 3, 4)
-        neighbour(3, 1, 3, 4, last_room[:, 2 * P - OVERLAP :])
+        neighbour(3, 1, 3, 4)
         neighbour(3, 2, 3, 4)
         second_layer(2, w2_codes, w2_scales, out_on_vector=True)
-        round_z(3, 2, 4, on_vector=True)
+        round_z(3, 3, 4, on_vector=True)
         turn_back(3)
-        second_layer(3, w2_codes, w2_scales)
+        second_layer(3, w2_codes, w2_scales, split=True)

@@ -50,19 +50,10 @@ def tile_picked_wlapl_gelu_l_kernel(
         def sb(shape, dtype, name, tag=""):
             return keep.tile(shape, dtype, name=name, tag=tag or name, align_bytes=ALIGN)
 
-        x_rows = sb([P, T // 4], I32, "x_rows")
-        for q in range(4):
-            nc.scalar.dma_start(
-                out=x_rows[32 * q : 32 * q + 4 * PASSES, :],
-                in_=x_scales[:, 4 * q : 4 * q + 4, :].bitcast(I32),
-            )
+        x_planes = sb([P, PASSES, T], U8, "x_planes")
+        nc.gpsimd.memset(x_planes[:].rearrange("p z c -> p (z c)").bitcast(I32), 0)
         zeros = sb([P, SPARE], F32, "zeros")
         nc.vector.memset(zeros[:], 0.0)
-        x_plane = sb([P, T], U8, "x_plane")
-        nc.vector.memset(x_plane[:].bitcast(I32), 0)
-        for q in range(4):
-            rows = slice(32 * q, 32 * q + 4 * PASSES)
-            nc.vector.tensor_copy(out=x_plane[rows, :].bitcast(I32), in_=x_rows[rows, :])
         h = [sb([P, T + SPARE], F32, f"h{t}") for t in range(H_TILES)]
         nc.scalar.activation(out=h[0][:, T:], in_=zeros[:], func=GELU)
         ident = sb([P, P], F32, "ident")
@@ -90,6 +81,9 @@ def tile_picked_wlapl_gelu_l_kernel(
             nc.sync.dma_start(offsets[d][:], pos[d])
 
         load_w1(0, 1)
+        scale_rows = x_scales.rearrange("z (q r) c -> r q z c", r=4)
+        for r in range(4):
+            nc.sync.dma_start(out=x_planes[r:P:32].bitcast(I32), in_=scale_rows[r].bitcast(I32))
         x_codes = [sb([P, T], U32, f"x_codes{z}") for z in range(PASSES)]
         for z in range(PASSES):
             nc.sync.dma_start(
@@ -126,7 +120,7 @@ def tile_picked_wlapl_gelu_l_kernel(
                         lhsT=codes[z].bitcast(FP8X4),
                         lhsT_scale=scales[z],
                         rhs=x_codes[z][:, cols].bitcast(FP8X4),
-                        rhs_scale=x_plane[4 * z :, cols],
+                        rhs_scale=x_planes[:, z, cols],
                         start=(z == 0),
                         stop=(z == PASSES - 1),
                     )
@@ -196,9 +190,20 @@ def tile_picked_wlapl_gelu_l_kernel(
             for b in range(b0, b1):
                 add_turned(t, b, term[:, (b - b0) * P : (b - b0 + 1) * P], False, d == D - 1)
 
-        z_words = [sb([P, 2 * P], F32, f"z_words{b}")[:] for b in range(V_BLOCKS)]
+        last_room = sb([P, 3 * P - OVERLAP], F32, "last_room")
+        z_words = [
+            room_before(3, 2, 2, 2 * P),
+            sb([P, 2 * P], F32, "z_words1")[:],
+            last_room[:, : 2 * P],
+            sb([P, 2 * P], F32, "z_words3")[:],
+        ]
         z_rows = [w.bitcast(BF16).rearrange("v (u p e) -> v u p e", u=2, e=2) for w in z_words]
-        z_grouped = [sb([P, 2 * P], F32, f"z_grouped{b}")[:] for b in range(V_BLOCKS)]
+        z_grouped = [
+            room_before(2, 0, 3, 2 * P),
+            room_before(2, 1, 3, 2 * P),
+            sb([P, 2 * P], F32, "z_grouped2")[:],
+            sb([P, 2 * P], F32, "z_grouped3")[:],
+        ]
 
         def round_z(b, t0, t1, on_vector=False):
             src = bank_of(t0, b)[:].rearrange("v (p u e) -> v u p e", u=2, e=2)[:, :, 32 * t0 : 32 * t1, :]
@@ -294,7 +299,7 @@ def tile_picked_wlapl_gelu_l_kernel(
             neighbour(2, d, 3, 4)
         round_z(3, 2, 3)
         neighbour(3, 0, 3, 4)
-        neighbour(3, 1, 3, 4)
+        neighbour(3, 1, 3, 4, last_room[:, 2 * P - OVERLAP :])
         neighbour(3, 2, 3, 4)
         second_layer(2, w2_codes, w2_scales, out_on_vector=True)
         round_z(3, 3, 4, on_vector=True)

@@ -26,8 +26,8 @@ M_TILES = N // P
 SPARE = 16
 ALIGN = 64
 OVERLAP = 16
-STRIP = H_TILES * T + T
-STEPS = [(0, 0, 4), (1, 0, 4), (2, 0, 2), (3, 0, 2), (2, 2, 3), (3, 2, 3), (2, 3, 4), (3, 3, 4)]
+STRIP = H_TILES * T + 2 * T
+STEPS = [(0, 0, 4), (1, 0, 4), (3, 0, 4), (2, 0, 2), (2, 2, 3), (2, 3, 4)]
 
 
 def interleave_views(grouped, raw):
@@ -61,18 +61,29 @@ def tile_picked_wlapl_gelu_l_kernel(
         for t in range(1, H_TILES):
             nc.gpsimd.memset(h[t][:, T:], 0.0)
 
+        strips = [sb([P, STRIP], F32, f"strip{d}") for d in range(D)]
+        head = {}
+        top = STRIP - T + OVERLAP
+        for t, b0, b1 in STEPS:
+            head[t, b0] = top - (b1 - b0) * P
+            top = head[t, b0] + OVERLAP
+
+        def room_before(t, d, b0, words, overlap=OVERLAP):
+            end = head[t, b0] + overlap
+            return strips[d][:, end - words : end]
+
         w1_rows = w1.rearrange("(z p j) c -> z p j c", z=PASSES, j=PACK)
         w1_raw = {}
 
-        def load_w1(t0, t1):
-            for z in range(PASSES):
-                raw = sb([P, PACK, (t1 - t0) * P], F32, f"w1_raw{t0}_{z}")
-                nc.sync.dma_start(out=raw[:], in_=w1_rows[z, :, :, t0 * P : t1 * P])
+        def load_w1(t0, t1, rooms, passes=(0, 1)):
+            for z in passes:
+                raw = rooms[z].rearrange("p (j c) -> p j c", j=PACK)
+                nc.sync.dma_start(out=raw, in_=w1_rows[z, :, :, t0 * P : t1 * P])
                 for t in range(t0, t1):
                     w1_raw[t, z] = raw[:, :, (t - t0) * P : (t - t0 + 1) * P]
 
         gate_raw = [sb([P, T], F32, f"gate_raw{d}") for d in range(D)]
-        minus_gate = [sb([P, T], F32, f"minus_gate{d}") for d in range(D)]
+        minus_h = [sb([P, T], F32, f"minus_h{t}") for t in range(H_TILES)]
         offsets = [lists.tile([P, T // 16], U16, name=f"offsets{d}") for d in range(D)]
         pos = [pos1, pos2, pos3]
 
@@ -80,34 +91,23 @@ def tile_picked_wlapl_gelu_l_kernel(
             nc.sync.dma_start(out=gate_raw[d][:], in_=gate[d])
             nc.sync.dma_start(offsets[d][:], pos[d])
 
-        load_w1(0, 1)
+        load_w1(0, 1, [sb([P, T], F32, f"w1_raw0_{z}")[:] for z in range(PASSES)])
         scale_rows = x_scales.rearrange("z (q r) c -> r q z c", r=4)
         for r in range(4):
             nc.sync.dma_start(out=x_planes[r:P:32].bitcast(I32), in_=scale_rows[r].bitcast(I32))
         x_codes = [sb([P, T], U32, f"x_codes{z}") for z in range(PASSES)]
-        for z in range(PASSES):
+        for z, c0, c1 in ((0, 0, T), (1, 0, T)):
             nc.sync.dma_start(
-                out=x_codes[z][:].bitcast(I32),
-                in_=x_words[z].rearrange("p n r -> p (n r)").bitcast(I32),
+                out=x_codes[z][:, c0:c1].bitcast(I32),
+                in_=x_words[z, :, c0:c1, :].rearrange("p n r -> p (n r)").bitcast(I32),
             )
         load_neighbour(0)
+        load_w1(1, 2, [minus_h[0][:], strips[1][:, STRIP - T :]])
         load_neighbour(1)
-        load_w1(1, 2)
         load_neighbour(2)
-        load_w1(2, 4)
-        w2_raw = sb([P, PACK, N], F32, "w2_raw")
-        nc.sync.dma_start(out=w2_raw[:], in_=w2.rearrange("(p j) n -> p j n", j=PACK))
-
-        strips = [sb([P, STRIP], F32, f"strip{d}") for d in range(D)]
-        head = {}
-        top = STRIP
-        for t, b0, b1 in STEPS:
-            head[t, b0] = top - (b1 - b0) * P
-            top = head[t, b0] + OVERLAP
-
-        def room_before(t, d, b0, words):
-            end = head[t, b0] + OVERLAP
-            return strips[d][:, end - words : end]
+        load_w1(2, 4, [sb([P, 2 * T], F32, "w1_raw23_0")[:], room_before(1, 1, 0, 2 * T)])
+        w2_raw = sb([P, PACK, N], F32, "w2_raw")[:]
+        nc.sync.dma_start(out=w2_raw, in_=w2.rearrange("(p j) n -> p j n", j=PACK))
 
         def hidden(t, codes, scales, pieces=1):
             width = T // pieces
@@ -144,11 +144,15 @@ def tile_picked_wlapl_gelu_l_kernel(
                 scales.append(s[:])
             hidden(0, codes, scales, pieces=2)
 
-        def later_hidden(t, flat):
+        def later_hidden(t, vector_passes=0):
+            flat = sb([P, PASSES * P * PACK], BF16, f"w1_grouped{t}")[:]
             g = flat.rearrange("p (z c j) -> p z c j", z=PASSES, j=PACK)
             for z in range(PASSES):
                 dst, src = interleave_views(g[:, z], w1_raw[t, z])
-                nc.scalar.copy(out=dst, in_=src)
+                if z < vector_passes:
+                    nc.vector.tensor_copy(out=dst, in_=src)
+                else:
+                    nc.scalar.copy(out=dst, in_=src)
             c = sb([P, PASSES * P], U32, f"w1_codes{t}")
             s = sb([P, PASSES * P], U8, f"w1_scales{t}")
             nc.vector.quantize_mx(
@@ -163,7 +167,7 @@ def tile_picked_wlapl_gelu_l_kernel(
         z_t = [sums.tile([P, H], F32, name=f"z_t{b}") for b in range(V_BLOCKS)]
 
         def bank_of(t, b):
-            return z_t[0] if (t, b) == (H_TILES - 1, V_BLOCKS - 1) else z_t[b]
+            return z_t[b]
 
         def add_turned(t, b, values, start, stop):
             nc.tensor.matmul(
@@ -176,34 +180,25 @@ def tile_picked_wlapl_gelu_l_kernel(
             )
 
         def neighbour(t, d, b0, b1, place=None):
+            if d == 0 and b0 == 0:
+                nc.scalar.activation(out=minus_h[t][:], in_=h[t][:, :T], func=COPY, scale=-1.0)
             if d == 0:
                 for b in range(b0, b1):
-                    add_turned(t, b, h[t][:, b * P : (b + 1) * P], True, False)
+                    add_turned(t, b, minus_h[t][:, b * P : (b + 1) * P], True, False)
             width = (b1 - b0) * P
             term = strips[d][:, head[t, b0] : head[t, b0] + width] if place is None else place
             nc.vector.tensor_tensor(
                 term,
                 h[t][:].indirect(offsets[d][:, b0 * P // 16 : b1 * P // 16]),
-                minus_gate[d][:, b0 * P : b1 * P],
+                gate_raw[d][:, b0 * P : b1 * P],
                 MULT,
             )
             for b in range(b0, b1):
                 add_turned(t, b, term[:, (b - b0) * P : (b - b0 + 1) * P], False, d == D - 1)
 
-        last_room = sb([P, 3 * P - OVERLAP], F32, "last_room")
-        z_words = [
-            room_before(3, 2, 2, 2 * P),
-            sb([P, 2 * P], F32, "z_words1")[:],
-            last_room[:, : 2 * P],
-            sb([P, 2 * P], F32, "z_words3")[:],
-        ]
+        z_words = [sb([P, 2 * P], F32, f"z_words{b}")[:] for b in range(V_BLOCKS)]
         z_rows = [w.bitcast(BF16).rearrange("v (u p e) -> v u p e", u=2, e=2) for w in z_words]
-        z_grouped = [
-            room_before(2, 0, 3, 2 * P),
-            room_before(2, 1, 3, 2 * P),
-            sb([P, 2 * P], F32, "z_grouped2")[:],
-            sb([P, 2 * P], F32, "z_grouped3")[:],
-        ]
+        z_grouped = [sb([P, 2 * P], F32, f"z_grouped{b}")[:] for b in range(V_BLOCKS)]
 
         def round_z(b, t0, t1, on_vector=False):
             src = bank_of(t0, b)[:].rearrange("v (p u e) -> v u p e", u=2, e=2)[:, :, 32 * t0 : 32 * t1, :]
@@ -257,51 +252,43 @@ def tile_picked_wlapl_gelu_l_kernel(
             nc.sync.dma_start(out=out_rows[:, :, b * P : (b + 1) * P], in_=result[:])
 
         first_hidden()
-        for d in range(2):
-            nc.vector.tensor_scalar_mul(minus_gate[d][:], gate_raw[d][:], -1.0)
+        later_hidden(1)
         neighbour(0, 0, 0, 4)
         neighbour(0, 1, 0, 4)
-        later_hidden(1, room_before(0, 2, 0, T).bitcast(BF16))
-        nc.scalar.activation(out=minus_gate[2][:], in_=gate_raw[2][:], func=COPY, scale=-1.0)
         neighbour(0, 2, 0, 4)
         neighbour(1, 0, 0, 4)
-        later_hidden(2, room_before(1, 1, 0, T).bitcast(BF16))
+        later_hidden(3)
         neighbour(1, 1, 0, 4)
-        later_hidden(3, room_before(1, 2, 0, T).bitcast(BF16))
         neighbour(1, 2, 0, 4)
-
-        w2_grouped = room_before(2, 1, 0, T).bitcast(BF16)
-        dst, src = interleave_views(w2_grouped.rearrange("p (n j) -> p n j", j=PACK), w2_raw[:])
-        nc.scalar.copy(out=dst, in_=src)
+        later_hidden(2)
         for b in range(V_BLOCKS):
             round_z(b, 0, 2)
-        neighbour(2, 0, 0, 2)
+        w2_grouped = sb([P, N * PACK], BF16, "w2_grouped")[:]
+        dst, src = interleave_views(w2_grouped.rearrange("p (n j) -> p n j", j=PACK), w2_raw)
+        nc.scalar.activation(out=dst, in_=src, func=COPY, scale=-1.0)
+        neighbour(3, 0, 0, 4)
         w2_codes = sb([P, N], U32, "w2_codes")
         w2_scales = sb([P, N], U8, "w2_scales")
         nc.vector.quantize_mx(out=w2_codes[:].bitcast(FP8X4), scales=w2_scales[:], in_=w2_grouped)
-        neighbour(2, 1, 0, 2)
-        neighbour(2, 2, 0, 2)
+        neighbour(3, 1, 0, 4)
+        neighbour(3, 2, 0, 4)
+        for b in range(V_BLOCKS):
+            round_z(b, 3, 4)
         for d in range(D):
-            neighbour(3, d, 0, 2)
-        round_z(0, 2, 4)
-        round_z(1, 2, 4)
+            neighbour(2, d, 0, 2)
+        round_z(0, 2, 3)
+        round_z(1, 2, 3)
         turn_back(0)
         turn_back(1)
         for d in range(D):
             neighbour(2, d, 2, 3)
-        for d in range(D):
-            neighbour(3, d, 2, 3)
-        round_z(2, 2, 4)
-        second_layer(0, w2_codes, w2_scales)
-        second_layer(1, w2_codes, w2_scales)
+        round_z(2, 2, 3)
         turn_back(2)
         for d in range(D):
             neighbour(2, d, 3, 4)
-        round_z(3, 2, 3)
-        neighbour(3, 0, 3, 4)
-        neighbour(3, 1, 3, 4, last_room[:, 2 * P - OVERLAP :])
-        neighbour(3, 2, 3, 4)
-        second_layer(2, w2_codes, w2_scales, out_on_vector=True)
-        round_z(3, 3, 4, on_vector=True)
+        second_layer(0, w2_codes, w2_scales)
+        second_layer(1, w2_codes, w2_scales)
+        round_z(3, 2, 3, on_vector=True)
         turn_back(3)
+        second_layer(2, w2_codes, w2_scales, out_on_vector=True)
         second_layer(3, w2_codes, w2_scales, split=True)

@@ -20,14 +20,11 @@ MULT = mybir.AluOpType.mult
 P = 128
 PACK = 4
 PASSES = K // (P * PACK)
-H_TILES = H // P
-V_BLOCKS = T // P
 M_TILES = N // P
 SPARE = 16
 ALIGN = 64
 OVERLAP = 16
-STRIP = H_TILES * T + 2 * T
-STEPS = [(0, 0, 4), (1, 0, 4), (3, 0, 4), (2, 0, 2), (2, 2, 3), (2, 3, 4)]
+A, B, C, E = 0, 1, 3, 2
 
 
 def interleave_views(grouped, raw):
@@ -44,251 +41,288 @@ def tile_picked_wlapl_gelu_l_kernel(
     with ExitStack() as ctx:
         lists = ctx.enter_context(tc.tile_pool(name="lists", bufs=1))
         keep = ctx.enter_context(tc.tile_pool(name="keep", bufs=1))
-        sums = ctx.enter_context(tc.psum_pool(name="sums", bufs=1))
-        work = ctx.enter_context(tc.psum_pool(name="work", bufs=4))
+        psum = ctx.enter_context(tc.psum_pool(name="psum", bufs=1))
 
         def sb(shape, dtype, name, tag=""):
             return keep.tile(shape, dtype, name=name, tag=tag or name, align_bytes=ALIGN)
+
+        def bank(k, shape, name):
+            return psum.tile(shape, F32, name=name, tag=f"bank{k}")
 
         x_planes = sb([P, PASSES, T], U8, "x_planes")
         nc.gpsimd.memset(x_planes[:].rearrange("p z c -> p (z c)").bitcast(I32), 0)
         zeros = sb([P, SPARE], F32, "zeros")
         nc.vector.memset(zeros[:], 0.0)
-        h = [sb([P, T + SPARE], F32, f"h{t}") for t in range(H_TILES)]
-        nc.scalar.activation(out=h[0][:, T:], in_=zeros[:], func=GELU)
+        h = [sb([P, T + SPARE], F32, f"h{t}") for t in range(4)]
+        nc.scalar.activation(out=h[A][:, T:], in_=zeros[:], func=GELU)
         ident = sb([P, P], F32, "ident")
         make_identity(nc, ident[:])
-        for t in range(1, H_TILES):
+        for t in (B, C, E):
             nc.gpsimd.memset(h[t][:, T:], 0.0)
-
-        strips = [sb([P, STRIP], F32, f"strip{d}") for d in range(D)]
-        head = {}
-        top = STRIP - T + OVERLAP
-        for t, b0, b1 in STEPS:
-            head[t, b0] = top - (b1 - b0) * P
-            top = head[t, b0] + OVERLAP
-
-        def room_before(t, d, b0, words, overlap=OVERLAP):
-            end = head[t, b0] + overlap
-            return strips[d][:, end - words : end]
 
         w1_rows = w1.rearrange("(z p j) c -> z p j c", z=PASSES, j=PACK)
         w1_raw = {}
 
-        def load_w1(t0, t1, rooms, passes=(0, 1)):
-            for z in passes:
-                raw = rooms[z].rearrange("p (j c) -> p j c", j=PACK)
-                nc.sync.dma_start(out=raw, in_=w1_rows[z, :, :, t0 * P : t1 * P])
-                for t in range(t0, t1):
-                    w1_raw[t, z] = raw[:, :, (t - t0) * P : (t - t0 + 1) * P]
+        def load_w1(t0, t1, z, room):
+            raw = room.rearrange("p (j c) -> p j c", j=PACK)
+            nc.sync.dma_start(out=raw, in_=w1_rows[z, :, :, t0 * P : t1 * P])
+            for t in range(t0, t1):
+                w1_raw[t, z] = raw[:, :, (t - t0) * P : (t - t0 + 1) * P]
 
-        gate_raw = [sb([P, T], F32, f"gate_raw{d}") for d in range(D)]
-        minus_h = [sb([P, T], F32, f"minus_h{t}") for t in range(H_TILES)]
-        offsets = [lists.tile([P, T // 16], U16, name=f"offsets{d}") for d in range(D)]
-        pos = [pos1, pos2, pos3]
+        strip_b = sb([P, 3 * T - 2 * OVERLAP], F32, "strip_b")
+        strip_ce = sb([P, 4 * T - 2 * OVERLAP], F32, "strip_ce")
+        places = {
+            (A, 2): strip_b[:, :T],
+            (A, 1): strip_b[:, 2 * T - 2 * OVERLAP :],
+            (B, 2): strip_ce[:, :T],
+            (B, 1): strip_ce[:, 3 * T - 2 * OVERLAP :],
+        }
 
-        def load_neighbour(d):
-            nc.sync.dma_start(out=gate_raw[d][:], in_=gate[d])
-            nc.sync.dma_start(offsets[d][:], pos[d])
-
-        load_w1(0, 1, [sb([P, T], F32, f"w1_raw0_{z}")[:] for z in range(PASSES)])
+        gate_cols = sb([P, D, 8], F32, "gate_cols")
+        nc.sync.dma_start(out=gate_cols[:, :, :PACK], in_=gate[:, 0, :].rearrange("d (p b) -> p d b", b=PACK))
+        load_w1(A, A + 1, 0, sb([P, T], F32, "w1_raw_a0")[:])
         scale_rows = x_scales.rearrange("z (q r) c -> r q z c", r=4)
         for r in range(4):
             nc.sync.dma_start(out=x_planes[r:P:32].bitcast(I32), in_=scale_rows[r].bitcast(I32))
-        x_codes = [sb([P, T], U32, f"x_codes{z}") for z in range(PASSES)]
-        for z, c0, c1 in ((0, 0, T), (1, 0, T)):
+        load_w1(A, A + 1, 1, sb([P, T], F32, "w1_raw_a1")[:])
+        x_first = sb([P, T], U32, "x_first")
+        x_second = [sb([P, T // 2], U32, f"x_second{i}") for i in range(2)]
+
+        def load_x(dst, z, c0, c1):
             nc.sync.dma_start(
-                out=x_codes[z][:, c0:c1].bitcast(I32),
-                in_=x_words[z, :, c0:c1, :].rearrange("p n r -> p (n r)").bitcast(I32),
+                out=dst.bitcast(I32), in_=x_words[z, :, c0:c1, :].rearrange("p n r -> p (n r)").bitcast(I32)
             )
-        load_neighbour(0)
-        load_w1(1, 2, [minus_h[0][:], strips[1][:, STRIP - T :]])
-        load_neighbour(1)
-        load_neighbour(2)
-        load_w1(2, 4, [sb([P, 2 * T], F32, "w1_raw23_0")[:], room_before(1, 1, 0, 2 * T)])
+
+        load_x(x_first[:], 0, 0, T)
+        for i in range(2):
+            load_x(x_second[i][:], 1, i * T // 2, (i + 1) * T // 2)
+        offsets = [lists.tile([P, T // 16], U16, name=f"offsets{d}") for d in range(D)]
+        nc.sync.dma_start(offsets[0][:], pos1)
+        load_w1(B, B + 1, 0, sb([P, T], F32, "w1_raw_b0")[:])
+        load_w1(B, B + 1, 1, strip_b[:, T - OVERLAP : 2 * T - OVERLAP])
+        nc.sync.dma_start(offsets[1][:], pos2)
+        nc.sync.dma_start(offsets[2][:], pos3)
+        load_w1(2, 4, 0, sb([P, 2 * T], F32, "w1_raw_ce0")[:])
+        load_w1(2, 4, 1, strip_ce[:, T - OVERLAP : 3 * T - OVERLAP])
         w2_raw = sb([P, PACK, N], F32, "w2_raw")[:]
         nc.sync.dma_start(out=w2_raw, in_=w2.rearrange("(p j) n -> p j n", j=PACK))
 
-        def hidden(t, codes, scales, pieces=1):
-            width = T // pieces
-            accs = [work.tile([P, width], F32, name=f"h_acc{t}_{i}", tag="work") for i in range(pieces)]
-            for z in range(PASSES):
-                for i in range(pieces):
-                    cols = slice(i * width, (i + 1) * width)
-                    nc.tensor.matmul_mx(
-                        out=accs[i][:],
-                        lhsT=codes[z].bitcast(FP8X4),
-                        lhsT_scale=scales[z],
-                        rhs=x_codes[z][:, cols].bitcast(FP8X4),
-                        rhs_scale=x_planes[:, z, cols],
-                        start=(z == 0),
-                        stop=(z == PASSES - 1),
-                    )
-            for i in range(pieces):
+        minus_gate = []
+        for d in range(D):
+            spread = bank(d, [P, PACK, P], f"spread{d}")
+            for b in range(PACK):
+                nc.tensor.transpose(spread[:, b, :], gate_cols[:, d, b : b + 1].to_broadcast([P, P]), ident[:])
+            g = sb([P, T], F32, f"minus_gate{d}")
+            nc.scalar.activation(
+                out=g[:].rearrange("p (n b) -> p n b", b=PACK),
+                in_=spread[:].rearrange("p b n -> p n b"),
+                func=COPY,
+                scale=-1.0,
+            )
+            minus_gate.append(g)
+
+        def x_codes(z, i):
+            if z == 0:
+                return x_first[:, i * T // 2 : (i + 1) * T // 2]
+            return x_second[i][:]
+
+        def hidden(t, codes, scales, banks, by_pass):
+            width = T // 2
+            accs = [bank(k, [P, width], f"h_acc{t}_{i}") for i, k in enumerate(banks)]
+            steps = [(z, i) for z in range(PASSES) for i in range(2)]
+            if not by_pass:
+                steps = [(z, i) for i in range(2) for z in range(PASSES)]
+            for z, i in steps:
+                nc.tensor.matmul_mx(
+                    out=accs[i][:],
+                    lhsT=codes[z].bitcast(FP8X4),
+                    lhsT_scale=scales[z],
+                    rhs=x_codes(z, i).bitcast(FP8X4),
+                    rhs_scale=x_planes[:, z, i * width : (i + 1) * width],
+                    start=(z == 0),
+                    stop=(z == PASSES - 1),
+                )
+            for i in range(2):
                 nc.scalar.activation(out=h[t][:, i * width : (i + 1) * width], in_=accs[i][:], func=GELU)
 
         def first_hidden():
-            codes, scales, grouped = [], [], []
+            codes, scales = [], []
             for z in range(PASSES):
-                g = sb([P, P, PACK], BF16, f"w1_grouped0_{z}")
-                dst, src = interleave_views(g[:], w1_raw[0, z])
+                g = sb([P, P, PACK], BF16, f"w1_grouped_a{z}")
+                dst, src = interleave_views(g[:], w1_raw[A, z])
                 nc.vector.tensor_copy(out=dst, in_=src)
-                grouped.append(g)
-            for z in range(PASSES):
-                c = sb([P, P], U32, f"w1_codes0_{z}")
-                s = sb([P, P], U8, f"w1_scales0_{z}")
-                nc.vector.quantize_mx(
-                    out=c[:].bitcast(FP8X4), scales=s[:], in_=grouped[z][:].rearrange("p c j -> p (c j)")
-                )
+                c = sb([P, P], U32, f"w1_codes_a{z}")
+                s = sb([P, P], U8, f"w1_scales_a{z}")
+                nc.vector.quantize_mx(out=c[:].bitcast(FP8X4), scales=s[:], in_=g[:].rearrange("p c j -> p (c j)"))
                 codes.append(c[:])
                 scales.append(s[:])
-            hidden(0, codes, scales, pieces=2)
+            hidden(A, codes, scales, (0, 1), True)
 
-        def later_hidden(t, vector_passes=0):
-            flat = sb([P, PASSES * P * PACK], BF16, f"w1_grouped{t}")[:]
+        def cast_w1(t, tag=""):
+            flat = sb([P, PASSES * P * PACK], BF16, f"w1_grouped{t}", tag)[:]
             g = flat.rearrange("p (z c j) -> p z c j", z=PASSES, j=PACK)
             for z in range(PASSES):
                 dst, src = interleave_views(g[:, z], w1_raw[t, z])
-                if z < vector_passes:
-                    nc.vector.tensor_copy(out=dst, in_=src)
-                else:
-                    nc.scalar.copy(out=dst, in_=src)
+                nc.scalar.copy(out=dst, in_=src)
+            return flat
+
+        def later_hidden(t, flat, banks):
             c = sb([P, PASSES * P], U32, f"w1_codes{t}")
             s = sb([P, PASSES * P], U8, f"w1_scales{t}")
-            nc.vector.quantize_mx(
-                out=c[:].bitcast(FP8X4), scales=s[:], in_=flat
-            )
+            nc.vector.quantize_mx(out=c[:].bitcast(FP8X4), scales=s[:], in_=flat)
             hidden(
                 t,
                 [c[:, z * P : (z + 1) * P] for z in range(PASSES)],
                 [s[:, z * P : (z + 1) * P] for z in range(PASSES)],
+                banks,
+                False,
             )
 
-        z_t = [sums.tile([P, H], F32, name=f"z_t{b}") for b in range(V_BLOCKS)]
+        def add_turned(dst, values, start=False, stop=False):
+            nc.tensor.matmul(out=dst, lhsT=values, rhs=ident[:], is_transpose=True, start=start, stop=stop)
 
-        def bank_of(t, b):
-            return z_t[b]
+        def own_value(t, b0, b1, acc, start):
+            for b in range(b0, b1):
+                add_turned(acc[:, b - b0, :], h[t][:, b * P : (b + 1) * P], start=start and b == b0)
 
-        def add_turned(t, b, values, start, stop):
-            nc.tensor.matmul(
-                out=bank_of(t, b)[:, t * P : (t + 1) * P],
-                lhsT=values,
-                rhs=ident[:],
-                is_transpose=True,
-                start=start,
-                stop=stop,
-            )
-
-        def neighbour(t, d, b0, b1, place=None):
-            if d == 0 and b0 == 0:
-                nc.scalar.activation(out=minus_h[t][:], in_=h[t][:, :T], func=COPY, scale=-1.0)
-            if d == 0:
-                for b in range(b0, b1):
-                    add_turned(t, b, minus_h[t][:, b * P : (b + 1) * P], True, False)
+        def neighbour(t, d, b0, b1, acc, stop):
             width = (b1 - b0) * P
-            term = strips[d][:, head[t, b0] : head[t, b0] + width] if place is None else place
+            term = places[t, d] if (t, d) in places else sb([P, width], F32, f"term{t}_{d}_{b0}")[:]
             nc.vector.tensor_tensor(
                 term,
                 h[t][:].indirect(offsets[d][:, b0 * P // 16 : b1 * P // 16]),
-                gate_raw[d][:, b0 * P : b1 * P],
+                minus_gate[d][:, b0 * P : b1 * P],
                 MULT,
             )
             for b in range(b0, b1):
-                add_turned(t, b, term[:, (b - b0) * P : (b - b0 + 1) * P], False, d == D - 1)
+                add_turned(acc[:, b - b0, :], term[:, (b - b0) * P : (b - b0 + 1) * P], stop=stop and b == b1 - 1)
 
-        z_words = [sb([P, 2 * P], F32, f"z_words{b}")[:] for b in range(V_BLOCKS)]
-        z_rows = [w.bitcast(BF16).rearrange("v (u p e) -> v u p e", u=2, e=2) for w in z_words]
-        z_grouped = [sb([P, 2 * P], F32, f"z_grouped{b}")[:] for b in range(V_BLOCKS)]
+        pieces = [(0, 2), (2, 3), (3, 4)]
+        z_words = {}
 
-        def round_z(b, t0, t1, on_vector=False):
-            src = bank_of(t0, b)[:].rearrange("v (p u e) -> v u p e", u=2, e=2)[:, :, 32 * t0 : 32 * t1, :]
-            dst = z_rows[b][:, :, 32 * t0 : 32 * t1, :]
-            if on_vector:
-                nc.vector.tensor_copy(out=dst, in_=src)
-            else:
-                nc.scalar.copy(out=dst, in_=src)
+        def round_z(t, b0, b1, acc):
+            src = acc.rearrange("v b (p u e) -> v b u p e", u=2, e=2)
+            rows = z_words[b0].bitcast(BF16).rearrange("v (b u p e) -> v b u p e", u=2, p=P, e=2)
+            nc.scalar.copy(out=rows[:, :, :, 32 * t : 32 * (t + 1), :], in_=src)
+
+        def round_all(t, first, acc):
+            for b0, b1 in pieces:
+                if b0 >= first:
+                    round_z(t, b0, b1, acc[:, b0 - first : b1 - first, :])
 
         out_rows = out.rearrange("(a m) v -> m a v", a=M_TILES)
+        z_grouped = {}
 
-        def turn_back(b):
-            words = z_words[b]
-            back = work.tile([P, 2, P], F32, name=f"back{b}", tag="work")
-            for u in range(2):
-                nc.tensor.transpose(back[:, u, :], words[:, u * P : (u + 1) * P], ident[:])
-            nc.scalar.copy(out=z_grouped[b].rearrange("p (v u) -> p v u", u=2), in_=back[:].rearrange("p u v -> p v u"))
-
-        def second_layer(b, w2_codes, w2_scales, out_on_vector=False, split=False):
-            grouped = z_grouped[b].bitcast(BF16)
-            codes = sb([P, P], U32, f"z_codes{b}")
-            scales = sb([P, P], U8, f"z_scales{b}")
-            nc.vector.quantize_mx(
-                out=codes[:].bitcast(FP8X4), scales=scales[:], in_=grouped
+        def turn_back(b0, b1, k):
+            n = b1 - b0
+            back = bank(k, [P, n, 2, P], f"back{b0}")
+            for b in range(n):
+                for u in range(2):
+                    nc.tensor.transpose(
+                        back[:, b, u, :], z_words[b0][:, (2 * b + u) * P : (2 * b + u + 1) * P], ident[:]
+                    )
+            z_grouped[b0] = sb([P, n * 2 * P], F32, f"z_grouped{b0}")[:]
+            nc.scalar.copy(
+                out=z_grouped[b0].rearrange("p (b v u) -> p b v u", b=n, u=2),
+                in_=back[:].rearrange("p b u v -> p b v u"),
             )
-            acc = work.tile([P, M_TILES, P], F32, name=f"out_acc{b}", tag="work")
-            places = [acc[:, 0, :], z_t[1][:, :P] if split else acc[:, 1, :]]
-            for a in range(M_TILES):
-                nc.tensor.matmul_mx(
-                    out=places[a],
-                    lhsT=w2_codes[:, a * P : (a + 1) * P].bitcast(FP8X4),
-                    lhsT_scale=w2_scales[:, a * P : (a + 1) * P],
-                    rhs=codes[:].bitcast(FP8X4),
-                    rhs_scale=scales[:],
-                    start=True,
-                    stop=True,
-                )
-            if split:
-                low = sb([P, P], F32, "result_low")
-                high = sb([P, P], F32, "result_high")
-                nc.vector.tensor_copy(out=low[:], in_=places[0])
-                nc.sync.dma_start(out=out_rows[:, 0, b * P : (b + 1) * P], in_=low[:])
-                nc.scalar.copy(out=high[:], in_=places[1])
-                nc.scalar.dma_start(out=out_rows[:, 1, b * P : (b + 1) * P], in_=high[:])
-                return
-            result = sb([P, M_TILES, P], F32, f"result{b}")
-            if out_on_vector:
-                nc.vector.tensor_copy(out=result[:], in_=acc[:])
-            else:
-                nc.scalar.copy(out=result[:], in_=acc[:])
-            nc.sync.dma_start(out=out_rows[:, :, b * P : (b + 1) * P], in_=result[:])
+
+        def quantize_z(b0, b1):
+            width = (b1 - b0) * P
+            codes = sb([P, width], U32, f"z_codes{b0}")
+            scales = sb([P, width], U8, f"z_scales{b0}")
+            nc.vector.quantize_mx(out=codes[:].bitcast(FP8X4), scales=scales[:], in_=z_grouped[b0].bitcast(BF16))
+            return codes, scales
+
+        def project(dst, a, z_mx):
+            nc.tensor.matmul_mx(
+                out=dst,
+                lhsT=w2_codes[:, a * P : (a + 1) * P].bitcast(FP8X4),
+                lhsT_scale=w2_scales[:, a * P : (a + 1) * P],
+                rhs=z_mx[0][:].bitcast(FP8X4),
+                rhs_scale=z_mx[1][:],
+                start=True,
+                stop=True,
+            )
 
         first_hidden()
-        later_hidden(1)
-        neighbour(0, 0, 0, 4)
-        neighbour(0, 1, 0, 4)
-        neighbour(0, 2, 0, 4)
-        neighbour(1, 0, 0, 4)
-        later_hidden(3)
-        neighbour(1, 1, 0, 4)
-        neighbour(1, 2, 0, 4)
-        later_hidden(2)
-        for b in range(V_BLOCKS):
-            round_z(b, 0, 2)
-        w2_grouped = sb([P, N * PACK], BF16, "w2_grouped")[:]
+        later_hidden(B, cast_w1(B, 'w1_codes_a1'), (3, 4))
+        sum_a = bank(5, [P, 4, P], "sum_a")
+        own_value(A, 0, 4, sum_a, True)
+        for d in range(D):
+            neighbour(A, d, 0, 4, sum_a, d == D - 1)
+        grouped_c = cast_w1(C, f"w1_codes{B}")
+        grouped_e = cast_w1(E, f"w1_scales{B}")
+        sum_b = bank(2, [P, 4, P], "sum_b")
+        own_value(B, 0, 4, sum_b, True)
+        neighbour(B, 0, 0, 4, sum_b, False)
+        later_hidden(C, grouped_c, (0, 1))
+        neighbour(B, 1, 0, 4, sum_b, False)
+        later_hidden(E, grouped_e, (3, 4))
+        neighbour(B, 2, 0, 4, sum_b, True)
+
+        w2_grouped = sb([P, N * PACK], BF16, "w2_grouped", f"w1_codes{E}")[:]
+        for (b0, b1), tag in zip(pieces, (f"w1_scales{B}", f"w1_codes{B}", "w1_raw_ce0")):
+            z_words[b0] = sb([P, (b1 - b0) * 2 * P], F32, f"z_words{b0}", tag)[:]
+        round_all(A, 0, sum_a[:])
+        round_all(B, 0, sum_b[:])
         dst, src = interleave_views(w2_grouped.rearrange("p (n j) -> p n j", j=PACK), w2_raw)
-        nc.scalar.activation(out=dst, in_=src, func=COPY, scale=-1.0)
-        neighbour(3, 0, 0, 4)
+        nc.scalar.copy(out=dst, in_=src)
+
+        sum_01 = bank(0, [P, 2, 2, P], "sum_01")
+        sum_c23 = bank(1, [P, 2, P], "sum_c23")
+        sum_e2 = bank(6, [P, 1, P], "sum_e2")
+        sum_e3 = bank(7, [P, 1, P], "sum_e3")
+        own_value(C, 0, 2, sum_01[:, 0], True)
+        own_value(C, 2, 4, sum_c23, True)
+        for d in range(D):
+            neighbour(C, d, 0, 2, sum_01[:, 0], False)
+        own_value(E, 0, 2, sum_01[:, 1], False)
+        own_value(E, 2, 3, sum_e2, True)
+        own_value(E, 3, 4, sum_e3, True)
+        for d in range(D):
+            neighbour(E, d, 0, 2, sum_01[:, 1], d == D - 1)
+        round_z(C, 0, 2, sum_01[:, 0])
+        round_z(E, 0, 2, sum_01[:, 1])
+        turn_back(0, 2, 3)
+        for d in range(D):
+            neighbour(C, d, 2, 4, sum_c23, d == D - 1)
+        round_all(C, 2, sum_c23[:])
+        for d in range(D):
+            neighbour(E, d, 2, 3, sum_e2, d == D - 1)
+        round_z(E, 2, 3, sum_e2[:])
+        for d in range(D):
+            neighbour(E, d, 3, 4, sum_e3, d == D - 1)
+        round_z(E, 3, 4, sum_e3[:])
+        turn_back(2, 3, 4)
+        turn_back(3, 4, 5)
+
         w2_codes = sb([P, N], U32, "w2_codes")
         w2_scales = sb([P, N], U8, "w2_scales")
         nc.vector.quantize_mx(out=w2_codes[:].bitcast(FP8X4), scales=w2_scales[:], in_=w2_grouped)
-        neighbour(3, 1, 0, 4)
-        neighbour(3, 2, 0, 4)
-        for b in range(V_BLOCKS):
-            round_z(b, 3, 4)
-        for d in range(D):
-            neighbour(2, d, 0, 2)
-        round_z(0, 2, 3)
-        round_z(1, 2, 3)
-        turn_back(0)
-        turn_back(1)
-        for d in range(D):
-            neighbour(2, d, 2, 3)
-        round_z(2, 2, 3)
-        turn_back(2)
-        for d in range(D):
-            neighbour(2, d, 3, 4)
-        second_layer(0, w2_codes, w2_scales)
-        second_layer(1, w2_codes, w2_scales)
-        round_z(3, 2, 3, on_vector=True)
-        turn_back(3)
-        second_layer(2, w2_codes, w2_scales, out_on_vector=True)
-        second_layer(3, w2_codes, w2_scales, split=True)
+        z01 = quantize_z(0, 2)
+        z2 = quantize_z(2, 3)
+        z3 = quantize_z(3, 4)
+
+        out_01 = bank(7, [P, M_TILES, 2 * P], "out_01")
+        for a in range(M_TILES):
+            project(out_01[:, a, :], a, z01)
+        out_2 = bank(2, [P, M_TILES, P], "out_2")
+        for a in range(M_TILES):
+            project(out_2[:, a, :], a, z2)
+        out_3 = [bank(a, [P, P], f"out_3{a}") for a in range(M_TILES)]
+        for a in range(M_TILES):
+            project(out_3[a][:], a, z3)
+
+        result_01 = sb([P, M_TILES, 2 * P], F32, "result_01")
+        nc.scalar.copy(out=result_01[:], in_=out_01[:])
+        nc.sync.dma_start(out=out_rows[:, :, : 2 * P], in_=result_01[:])
+        result_2 = sb([P, M_TILES, P], F32, "result_2")
+        nc.vector.tensor_copy(out=result_2[:], in_=out_2[:])
+        nc.sync.dma_start(out=out_rows[:, :, 2 * P : 3 * P], in_=result_2[:])
+        low = sb([P, P], F32, "result_low")
+        high = sb([P, P], F32, "result_high")
+        nc.vector.tensor_copy(out=low[:], in_=out_3[0][:])
+        nc.sync.dma_start(out=out_rows[:, 0, 3 * P :], in_=low[:])
+        nc.scalar.copy(out=high[:], in_=out_3[1][:])
+        nc.scalar.dma_start(out=out_rows[:, 1, 3 * P :], in_=high[:])

@@ -69,11 +69,11 @@ def tile_picked_wlapl_gelu_l_kernel(
             for t in range(t0, t1):
                 w1_raw[t, z] = raw[:, :, (t - t0) * P : (t - t0 + 1) * P]
 
-        strip_b = sb([P, 3 * T - 2 * OVERLAP], F32, "strip_b")
+        strip_b = sb([P, 4 * T - 3 * OVERLAP], F32, "strip_b")
         strip_ce = sb([P, 4 * T - 2 * OVERLAP], F32, "strip_ce")
         places = {
             (A, 2): strip_b[:, :T],
-            (A, 1): strip_b[:, 2 * T - 2 * OVERLAP :],
+            (A, 1): strip_b[:, 2 * T - 2 * OVERLAP : 3 * T - 2 * OVERLAP],
             (B, 2): strip_ce[:, :T],
             (B, 1): strip_ce[:, 3 * T - 2 * OVERLAP :],
         }
@@ -158,22 +158,28 @@ def tile_picked_wlapl_gelu_l_kernel(
                 scales.append(s[:])
             hidden(A, codes, scales, (0, 1), True)
 
+        def slot(t, z):
+            return 1 - z if t == C else z
+
         def cast_w1(t, tag=""):
-            flat = sb([P, PASSES * P * PACK], BF16, f"w1_grouped{t}", tag)[:]
+            if t == C:
+                flat = strip_b[:, 3 * T - 3 * OVERLAP :].bitcast(BF16)
+            else:
+                flat = sb([P, PASSES * P * PACK], BF16, f"w1_grouped{t}", tag)[:]
             g = flat.rearrange("p (z c j) -> p z c j", z=PASSES, j=PACK)
             for z in range(PASSES):
-                dst, src = interleave_views(g[:, z], w1_raw[t, z])
+                dst, src = interleave_views(g[:, slot(t, z)], w1_raw[t, z])
                 nc.scalar.copy(out=dst, in_=src)
             return flat
 
         def later_hidden(t, flat, banks):
-            c = sb([P, PASSES * P], U32, f"w1_codes{t}")
+            c = sb([P, PASSES * P], U32, f"w1_codes{t}")[:]
             s = sb([P, PASSES * P], U8, f"w1_scales{t}")
-            nc.vector.quantize_mx(out=c[:].bitcast(FP8X4), scales=s[:], in_=flat)
+            nc.vector.quantize_mx(out=c.bitcast(FP8X4), scales=s[:], in_=flat)
             hidden(
                 t,
-                [c[:, z * P : (z + 1) * P] for z in range(PASSES)],
-                [s[:, z * P : (z + 1) * P] for z in range(PASSES)],
+                [c[:, slot(t, z) * P : (slot(t, z) + 1) * P] for z in range(PASSES)],
+                [s[:, slot(t, z) * P : (slot(t, z) + 1) * P] for z in range(PASSES)],
                 banks,
                 False,
             )
@@ -185,7 +191,7 @@ def tile_picked_wlapl_gelu_l_kernel(
             for b in range(b0, b1):
                 add_turned(acc[:, b - b0, :], h[t][:, b * P : (b + 1) * P], start=start and b == b0)
 
-        def neighbour(t, d, b0, b1, acc, stop):
+        def neighbour(t, d, b0, b1, acc, stop, acc_high=None):
             width = (b1 - b0) * P
             term = places[t, d] if (t, d) in places else sb([P, width], F32, f"term{t}_{d}_{b0}")[:]
             nc.vector.tensor_tensor(
@@ -195,15 +201,17 @@ def tile_picked_wlapl_gelu_l_kernel(
                 MULT,
             )
             for b in range(b0, b1):
-                add_turned(acc[:, b - b0, :], term[:, (b - b0) * P : (b - b0 + 1) * P], stop=stop and b == b1 - 1)
+                dst = acc_high[b] if acc_high and b in acc_high else acc[:, b - b0, :]
+                add_turned(dst, term[:, (b - b0) * P : (b - b0 + 1) * P], stop=stop and (b == b1 - 1 or t == E))
 
         pieces = [(0, 2), (2, 3), (3, 4)]
         z_words = {}
 
-        def round_z(t, b0, b1, acc):
+        def round_z(t, b0, b1, acc, first=None):
+            first = b0 if first is None else first
             src = acc.rearrange("v b (p u e) -> v b u p e", u=2, e=2)
-            rows = z_words[b0].bitcast(BF16).rearrange("v (b u p e) -> v b u p e", u=2, p=P, e=2)
-            nc.scalar.copy(out=rows[:, :, :, 32 * t : 32 * (t + 1), :], in_=src)
+            rows = z_words[first].bitcast(BF16).rearrange("v (b u p e) -> v b u p e", u=2, p=P, e=2)
+            nc.scalar.copy(out=rows[:, b0 - first : b1 - first, :, 32 * t : 32 * (t + 1), :], in_=src)
 
         def round_all(t, first, acc):
             for b0, b1 in pieces:
@@ -251,7 +259,7 @@ def tile_picked_wlapl_gelu_l_kernel(
         own_value(A, 0, 4, sum_a, True)
         for d in range(D):
             neighbour(A, d, 0, 4, sum_a, d == D - 1)
-        grouped_c = cast_w1(C, f"w1_codes{B}")
+        grouped_c = cast_w1(C)
         grouped_e = cast_w1(E, f"w1_scales{B}")
         sum_b = bank(2, [P, 4, P], "sum_b")
         own_value(B, 0, 4, sum_b, True)
@@ -262,36 +270,41 @@ def tile_picked_wlapl_gelu_l_kernel(
         neighbour(B, 2, 0, 4, sum_b, True)
 
         w2_grouped = sb([P, N * PACK], BF16, "w2_grouped", f"w1_codes{E}")[:]
-        for (b0, b1), tag in zip(pieces, (f"w1_scales{B}", f"w1_codes{B}", "w1_raw_ce0")):
+        for (b0, b1), tag in zip(pieces, (f"w1_scales{B}", f"w1_scales{C}", "w1_raw_ce0")):
             z_words[b0] = sb([P, (b1 - b0) * 2 * P], F32, f"z_words{b0}", tag)[:]
         round_all(A, 0, sum_a[:])
         round_all(B, 0, sum_b[:])
         dst, src = interleave_views(w2_grouped.rearrange("p (n j) -> p n j", j=PACK), w2_raw)
         nc.scalar.copy(out=dst, in_=src)
 
-        sum_01 = bank(0, [P, 2, 2, P], "sum_01")
+        sum_c01 = bank(0, [P, 2, P], "sum_c01")
+        sum_e0 = bank(2, [P, 1, P], "sum_e0")
+        sum_e1 = bank(6, [P, 1, P], "sum_e1")
         sum_c23 = bank(1, [P, 2, P], "sum_c23")
-        sum_e2 = bank(6, [P, 1, P], "sum_e2")
-        sum_e3 = bank(7, [P, 1, P], "sum_e3")
-        own_value(C, 0, 2, sum_01[:, 0], True)
+        own_value(C, 0, 2, sum_c01, True)
         own_value(C, 2, 4, sum_c23, True)
+        for d in range(2):
+            neighbour(C, d, 0, 4, sum_c01, False, {2: sum_c23[:, 0, :], 3: sum_c23[:, 1, :]})
+        neighbour(C, 2, 0, 2, sum_c01, True)
+        round_z(C, 0, 2, sum_c01[:])
+        own_value(E, 0, 1, sum_e0, True)
+        own_value(E, 1, 2, sum_e1, True)
         for d in range(D):
-            neighbour(C, d, 0, 2, sum_01[:, 0], False)
-        own_value(E, 0, 2, sum_01[:, 1], False)
+            neighbour(E, d, 0, 2, sum_e0, d == D - 1, {1: sum_e1[:, 0, :]})
+        round_z(E, 0, 1, sum_e0[:])
+        round_z(E, 1, 2, sum_e1[:], 0)
+        turn_back(0, 2, 3)
+        sum_e2 = bank(2, [P, 1, P], "sum_e2")
+        sum_e3 = bank(6, [P, 1, P], "sum_e3")
         own_value(E, 2, 3, sum_e2, True)
         own_value(E, 3, 4, sum_e3, True)
-        for d in range(D):
-            neighbour(E, d, 0, 2, sum_01[:, 1], d == D - 1)
-        round_z(C, 0, 2, sum_01[:, 0])
-        round_z(E, 0, 2, sum_01[:, 1])
-        turn_back(0, 2, 3)
-        for d in range(D):
-            neighbour(C, d, 2, 4, sum_c23, d == D - 1)
+        neighbour(C, 2, 2, 4, sum_c23, True)
         round_all(C, 2, sum_c23[:])
-        for d in range(D):
+        neighbour(E, 0, 2, 4, sum_e2, False, {3: sum_e3[:, 0, :]})
+        for d in (1, 2):
             neighbour(E, d, 2, 3, sum_e2, d == D - 1)
         round_z(E, 2, 3, sum_e2[:])
-        for d in range(D):
+        for d in (1, 2):
             neighbour(E, d, 3, 4, sum_e3, d == D - 1)
         round_z(E, 3, 4, sum_e3[:])
         turn_back(2, 3, 4)
@@ -304,9 +317,9 @@ def tile_picked_wlapl_gelu_l_kernel(
         z2 = quantize_z(2, 3)
         z3 = quantize_z(3, 4)
 
-        out_01 = bank(7, [P, M_TILES, 2 * P], "out_01")
+        out_01 = [bank(k, [P, 2 * P], f"out_01{k}") for k in (6, 5)]
         for a in range(M_TILES):
-            project(out_01[:, a, :], a, z01)
+            project(out_01[a][:], a, z01)
         out_2 = bank(2, [P, M_TILES, P], "out_2")
         for a in range(M_TILES):
             project(out_2[:, a, :], a, z2)
@@ -314,11 +327,15 @@ def tile_picked_wlapl_gelu_l_kernel(
         for a in range(M_TILES):
             project(out_3[a][:], a, z3)
 
-        result_01 = sb([P, M_TILES, 2 * P], F32, "result_01")
-        nc.scalar.copy(out=result_01[:], in_=out_01[:])
-        nc.sync.dma_start(out=out_rows[:, :, : 2 * P], in_=result_01[:])
+        for a in range(M_TILES):
+            result_01 = sb([P, 2 * P], F32, f"result_01{a}")
+            if a == 0:
+                nc.scalar.copy(out=result_01[:], in_=out_01[a][:])
+            else:
+                nc.vector.tensor_copy(out=result_01[:], in_=out_01[a][:])
+            nc.sync.dma_start(out=out_rows[:, a, : 2 * P], in_=result_01[:])
         result_2 = sb([P, M_TILES, P], F32, "result_2")
-        nc.vector.tensor_copy(out=result_2[:], in_=out_2[:])
+        nc.scalar.copy(out=result_2[:], in_=out_2[:])
         nc.sync.dma_start(out=out_rows[:, :, 2 * P : 3 * P], in_=result_2[:])
         low = sb([P, P], F32, "result_low")
         high = sb([P, P], F32, "result_high")

@@ -69,13 +69,16 @@ def tile_picked_wlapl_gelu_l_kernel(
             for t in range(t0, t1):
                 w1_raw[t, z] = raw[:, :, (t - t0) * P : (t - t0 + 1) * P]
 
-        strip_b = sb([P, 4 * T - 3 * OVERLAP], F32, "strip_b")
+        half = T // 2
+        strip_b0 = sb([P, T + half - OVERLAP], F32, "strip_b0")
+        strip_b = sb([P, 3 * T + half - 3 * OVERLAP], F32, "strip_b")
         strip_ce = sb([P, 4 * T - 2 * OVERLAP], F32, "strip_ce")
         places = {
-            (A, 2): strip_b[:, :T],
-            (A, 1): strip_b[:, 2 * T - 2 * OVERLAP : 3 * T - 2 * OVERLAP],
-            (B, 2): strip_ce[:, :T],
-            (B, 1): strip_ce[:, 3 * T - 2 * OVERLAP :],
+            (A, 1, 0): strip_b0[:, T - OVERLAP :],
+            (A, 2, 0): strip_b[:, :T],
+            (A, 1, 2): strip_b[:, 2 * T - 2 * OVERLAP : 2 * T + half - 2 * OVERLAP],
+            (B, 2, 0): strip_ce[:, :T],
+            (B, 1, 0): strip_ce[:, 3 * T - 2 * OVERLAP :],
         }
 
         gate_cols = sb([P, D, 8], F32, "gate_cols")
@@ -98,9 +101,9 @@ def tile_picked_wlapl_gelu_l_kernel(
             load_x(x_second[i][:], 1, i * T // 2, (i + 1) * T // 2)
         offsets = [lists.tile([P, T // 16], U16, name=f"offsets{d}") for d in range(D)]
         nc.sync.dma_start(offsets[0][:], pos1)
-        load_w1(B, B + 1, 0, sb([P, T], F32, "w1_raw_b0")[:])
-        load_w1(B, B + 1, 1, strip_b[:, T - OVERLAP : 2 * T - OVERLAP])
+        load_w1(B, B + 1, 0, strip_b0[:, :T])
         nc.sync.dma_start(offsets[1][:], pos2)
+        load_w1(B, B + 1, 1, strip_b[:, T - OVERLAP : 2 * T - OVERLAP])
         nc.sync.dma_start(offsets[2][:], pos3)
         load_w1(2, 4, 0, sb([P, 2 * T], F32, "w1_raw_ce0")[:])
         load_w1(2, 4, 1, strip_ce[:, T - OVERLAP : 3 * T - OVERLAP])
@@ -145,25 +148,25 @@ def tile_picked_wlapl_gelu_l_kernel(
             for i in range(2):
                 nc.scalar.activation(out=h[t][:, i * width : (i + 1) * width], in_=accs[i][:], func=GELU)
 
-        def first_hidden():
+        def early_hidden(t, cast, tags, banks):
             codes, scales = [], []
             for z in range(PASSES):
-                g = sb([P, P, PACK], BF16, f"w1_grouped_a{z}")
-                dst, src = interleave_views(g[:], w1_raw[A, z])
-                nc.vector.tensor_copy(out=dst, in_=src)
-                c = sb([P, P], U32, f"w1_codes_a{z}")
-                s = sb([P, P], U8, f"w1_scales_a{z}")
+                g = sb([P, P, PACK], BF16, f"w1_grouped{t}_{z}", tags[z])
+                dst, src = interleave_views(g[:], w1_raw[t, z])
+                cast(out=dst, in_=src)
+                c = sb([P, P], U32, f"w1_codes{t}_{z}")
+                s = sb([P, P], U8, f"w1_scales{t}_{z}")
                 nc.vector.quantize_mx(out=c[:].bitcast(FP8X4), scales=s[:], in_=g[:].rearrange("p c j -> p (c j)"))
                 codes.append(c[:])
                 scales.append(s[:])
-            hidden(A, codes, scales, (0, 1), True)
+            hidden(t, codes, scales, banks, True)
 
         def slot(t, z):
             return 1 - z if t == C else z
 
         def cast_w1(t, tag=""):
             if t == C:
-                flat = strip_b[:, 3 * T - 3 * OVERLAP :].bitcast(BF16)
+                flat = strip_b[:, 2 * T + half - 3 * OVERLAP :].bitcast(BF16)
             else:
                 flat = sb([P, PASSES * P * PACK], BF16, f"w1_grouped{t}", tag)[:]
             g = flat.rearrange("p (z c j) -> p z c j", z=PASSES, j=PACK)
@@ -187,13 +190,15 @@ def tile_picked_wlapl_gelu_l_kernel(
         def add_turned(dst, values, start=False, stop=False):
             nc.tensor.matmul(out=dst, lhsT=values, rhs=ident[:], is_transpose=True, start=start, stop=stop)
 
-        def own_value(t, b0, b1, acc, start):
+        def own_value(t, b0, b1, acc, start, stop=False):
             for b in range(b0, b1):
-                add_turned(acc[:, b - b0, :], h[t][:, b * P : (b + 1) * P], start=start and b == b0)
+                add_turned(
+                    acc[:, b - b0, :], h[t][:, b * P : (b + 1) * P], start=start and b == b0, stop=stop and b == b1 - 1
+                )
 
-        def neighbour(t, d, b0, b1, acc, stop, acc_high=None):
+        def neighbour(t, d, b0, b1, acc, stop, acc_high=None, start=False):
             width = (b1 - b0) * P
-            term = places[t, d] if (t, d) in places else sb([P, width], F32, f"term{t}_{d}_{b0}")[:]
+            term = places[t, d, b0] if (t, d, b0) in places else sb([P, width], F32, f"term{t}_{d}_{b0}")[:]
             nc.vector.tensor_tensor(
                 term,
                 h[t][:].indirect(offsets[d][:, b0 * P // 16 : b1 * P // 16]),
@@ -202,7 +207,12 @@ def tile_picked_wlapl_gelu_l_kernel(
             )
             for b in range(b0, b1):
                 dst = acc_high[b] if acc_high and b in acc_high else acc[:, b - b0, :]
-                add_turned(dst, term[:, (b - b0) * P : (b - b0 + 1) * P], stop=stop and (b == b1 - 1 or t == E))
+                add_turned(
+                    dst,
+                    term[:, (b - b0) * P : (b - b0 + 1) * P],
+                    start=start and b == b0,
+                    stop=stop and (b == b1 - 1 or t == E),
+                )
 
         pieces = [(0, 2), (2, 3), (3, 4)]
         z_words = {}
@@ -253,24 +263,26 @@ def tile_picked_wlapl_gelu_l_kernel(
                 stop=True,
             )
 
-        first_hidden()
-        later_hidden(B, cast_w1(B, 'w1_codes_a1'), (3, 4))
+        early_hidden(A, nc.vector.tensor_copy, ("", ""), (0, 1))
+        early_hidden(B, nc.scalar.copy, (f"w1_codes{A}_1", f"w1_scales{A}_1"), (3, 4))
         sum_a = bank(5, [P, 4, P], "sum_a")
         own_value(A, 0, 4, sum_a, True)
-        for d in range(D):
-            neighbour(A, d, 0, 4, sum_a, d == D - 1)
+        neighbour(A, 0, 0, 4, sum_a, False)
+        neighbour(A, 1, 0, 2, sum_a, False)
+        neighbour(A, 1, 2, 4, sum_a[:, 2:], False)
+        neighbour(A, 2, 0, 4, sum_a, True)
         grouped_c = cast_w1(C)
-        grouped_e = cast_w1(E, f"w1_scales{B}")
+        grouped_e = cast_w1(E, f"w1_scales{B}_1")
         sum_b = bank(2, [P, 4, P], "sum_b")
-        own_value(B, 0, 4, sum_b, True)
-        neighbour(B, 0, 0, 4, sum_b, False)
+        neighbour(B, 0, 0, 4, sum_b, False, start=True)
         later_hidden(C, grouped_c, (0, 1))
         neighbour(B, 1, 0, 4, sum_b, False)
         later_hidden(E, grouped_e, (3, 4))
-        neighbour(B, 2, 0, 4, sum_b, True)
+        neighbour(B, 2, 0, 4, sum_b, False)
+        own_value(B, 0, 4, sum_b, False, True)
 
         w2_grouped = sb([P, N * PACK], BF16, "w2_grouped", f"w1_codes{E}")[:]
-        for (b0, b1), tag in zip(pieces, (f"w1_scales{B}", f"w1_scales{C}", "w1_raw_ce0")):
+        for (b0, b1), tag in zip(pieces, (f"w1_scales{B}_1", f"w1_scales{C}", "w1_raw_ce0")):
             z_words[b0] = sb([P, (b1 - b0) * 2 * P], F32, f"z_words{b0}", tag)[:]
         round_all(A, 0, sum_a[:])
         round_all(B, 0, sum_b[:])

@@ -23,8 +23,7 @@ PASSES = K // (P * PACK)
 M_TILES = N // P
 SPARE = 16
 ALIGN = 64
-OVERLAP = 16
-A, B, C, E = 0, 1, 3, 2
+A, B, C, E = 0, 1, 2, 3
 
 
 def interleave_views(grouped, raw):
@@ -62,51 +61,43 @@ def tile_picked_wlapl_gelu_l_kernel(
 
         w1_rows = w1.rearrange("(z p j) c -> z p j c", z=PASSES, j=PACK)
         w1_raw = {}
-
-        def load_w1(t0, t1, z, room):
-            raw = room.rearrange("p (j c) -> p j c", j=PACK)
-            nc.sync.dma_start(out=raw, in_=w1_rows[z, :, :, t0 * P : t1 * P])
-            for t in range(t0, t1):
-                w1_raw[t, z] = raw[:, :, (t - t0) * P : (t - t0 + 1) * P]
-
         half = T // 2
-        strip_b0 = sb([P, T + half - OVERLAP], F32, "strip_b0")
-        strip_b = sb([P, 3 * T + half - 3 * OVERLAP], F32, "strip_b")
-        strip_ce = sb([P, 4 * T - 2 * OVERLAP], F32, "strip_ce")
-        places = {
-            (A, 1, 0): strip_b0[:, T - OVERLAP :],
-            (A, 2, 0): strip_b[:, :T],
-            (A, 1, 2): strip_b[:, 2 * T - 2 * OVERLAP : 2 * T + half - 2 * OVERLAP],
-            (B, 2, 0): strip_ce[:, :T],
-            (B, 1, 0): strip_ce[:, 3 * T - 2 * OVERLAP :],
-        }
+
+        def load_w1(t, z, room):
+            w1_raw[t, z] = room.rearrange("p (j c) -> p j c", j=PACK)
+            nc.sync.dma_start(out=w1_raw[t, z], in_=w1_rows[z, :, :, t * P : (t + 1) * P])
+
+        strip = sb([P, 2 * T + half], F32, "strip")
+        rooms = {t: sb([P, T], F32, f"room{t}")[:] for t in (C, E)}
 
         gate_cols = sb([P, D, 8], F32, "gate_cols")
         nc.sync.dma_start(out=gate_cols[:, :, :PACK], in_=gate[:, 0, :].rearrange("d (p b) -> p d b", b=PACK))
-        load_w1(A, A + 1, 0, sb([P, T], F32, "w1_raw_a0")[:])
+        load_w1(A, 0, sb([P, T], F32, "w1_raw_a0")[:])
         scale_rows = x_scales.rearrange("z (q r) c -> r q z c", r=4)
         for r in range(4):
             nc.sync.dma_start(out=x_planes[r:P:32].bitcast(I32), in_=scale_rows[r].bitcast(I32))
-        load_w1(A, A + 1, 1, sb([P, T], F32, "w1_raw_a1")[:])
-        x_first = sb([P, T], U32, "x_first")
-        x_second = [sb([P, T // 2], U32, f"x_second{i}") for i in range(2)]
+        load_w1(A, 1, sb([P, T], F32, "w1_raw_a1")[:])
+        x_codes = [sb([P, T], U32, f"x_codes{z}") for z in range(PASSES)]
 
-        def load_x(dst, z, c0, c1):
+        def load_x(z, c0, c1):
             nc.sync.dma_start(
-                out=dst.bitcast(I32), in_=x_words[z, :, c0:c1, :].rearrange("p n r -> p (n r)").bitcast(I32)
+                out=x_codes[z][:, c0:c1].bitcast(I32),
+                in_=x_words[z, :, c0:c1, :].rearrange("p n r -> p (n r)").bitcast(I32),
             )
 
-        load_x(x_first[:], 0, 0, T)
-        for i in range(2):
-            load_x(x_second[i][:], 1, i * T // 2, (i + 1) * T // 2)
+        load_x(0, 0, T)
+        load_x(1, 0, half)
+        load_x(1, half, T)
         offsets = [lists.tile([P, T // 16], U16, name=f"offsets{d}") for d in range(D)]
         nc.sync.dma_start(offsets[0][:], pos1)
-        load_w1(B, B + 1, 0, strip_b0[:, :T])
-        nc.sync.dma_start(offsets[1][:], pos2)
-        load_w1(B, B + 1, 1, strip_b[:, T - OVERLAP : 2 * T - OVERLAP])
+        load_w1(B, 0, sb([P, T], F32, "w1_raw_b0")[:])
+        load_w1(B, 1, strip[:, T - P : 2 * T - P])
         nc.sync.dma_start(offsets[2][:], pos3)
-        load_w1(2, 4, 0, sb([P, 2 * T], F32, "w1_raw_ce0")[:])
-        load_w1(2, 4, 1, strip_ce[:, T - OVERLAP : 3 * T - OVERLAP])
+        nc.sync.dma_start(offsets[1][:], pos2)
+        load_w1(C, 0, sb([P, T], F32, "w1_raw_c0")[:])
+        load_w1(C, 1, rooms[C])
+        load_w1(E, 0, sb([P, T], F32, "w1_raw_e0")[:])
+        load_w1(E, 1, rooms[E])
         w2_raw = sb([P, PACK, N], F32, "w2_raw")[:]
         nc.sync.dma_start(out=w2_raw, in_=w2.rearrange("(p j) n -> p j n", j=PACK))
 
@@ -124,109 +115,104 @@ def tile_picked_wlapl_gelu_l_kernel(
             )
             minus_gate.append(g)
 
-        def x_codes(z, i):
-            if z == 0:
-                return x_first[:, i * T // 2 : (i + 1) * T // 2]
-            return x_second[i][:]
+        grouped, codes, scales, accs = {}, {}, {}, {}
 
-        def hidden(t, codes, scales, banks, by_pass):
-            width = T // 2
-            accs = [bank(k, [P, width], f"h_acc{t}_{i}") for i, k in enumerate(banks)]
-            steps = [(z, i) for z in range(PASSES) for i in range(2)]
-            if not by_pass:
-                steps = [(z, i) for i in range(2) for z in range(PASSES)]
-            for z, i in steps:
-                nc.tensor.matmul_mx(
-                    out=accs[i][:],
-                    lhsT=codes[z].bitcast(FP8X4),
-                    lhsT_scale=scales[z],
-                    rhs=x_codes(z, i).bitcast(FP8X4),
-                    rhs_scale=x_planes[:, z, i * width : (i + 1) * width],
-                    start=(z == 0),
-                    stop=(z == PASSES - 1),
-                )
-            for i in range(2):
-                nc.scalar.activation(out=h[t][:, i * width : (i + 1) * width], in_=accs[i][:], func=GELU)
+        def cast_w1(t, z, copy, tag=""):
+            grouped[t, z] = sb([P, P, PACK], BF16, f"w1_grouped{t}_{z}", tag)
+            dst, src = interleave_views(grouped[t, z][:], w1_raw[t, z])
+            copy(out=dst, in_=src)
 
-        def early_hidden(t, cast, tags, banks):
-            codes, scales = [], []
-            for z in range(PASSES):
-                g = sb([P, P, PACK], BF16, f"w1_grouped{t}_{z}", tags[z])
-                dst, src = interleave_views(g[:], w1_raw[t, z])
-                cast(out=dst, in_=src)
-                c = sb([P, P], U32, f"w1_codes{t}_{z}")
-                s = sb([P, P], U8, f"w1_scales{t}_{z}")
-                nc.vector.quantize_mx(out=c[:].bitcast(FP8X4), scales=s[:], in_=g[:].rearrange("p c j -> p (c j)"))
-                codes.append(c[:])
-                scales.append(s[:])
-            hidden(t, codes, scales, banks, True)
-
-        def slot(t, z):
-            return 1 - z if t == C else z
-
-        def cast_w1(t, tag=""):
-            if t == C:
-                flat = strip_b[:, 2 * T + half - 3 * OVERLAP :].bitcast(BF16)
-            else:
-                flat = sb([P, PASSES * P * PACK], BF16, f"w1_grouped{t}", tag)[:]
-            g = flat.rearrange("p (z c j) -> p z c j", z=PASSES, j=PACK)
-            for z in range(PASSES):
-                dst, src = interleave_views(g[:, slot(t, z)], w1_raw[t, z])
-                nc.scalar.copy(out=dst, in_=src)
-            return flat
-
-        def later_hidden(t, flat, banks):
-            c = sb([P, PASSES * P], U32, f"w1_codes{t}")[:]
-            s = sb([P, PASSES * P], U8, f"w1_scales{t}")
-            nc.vector.quantize_mx(out=c.bitcast(FP8X4), scales=s[:], in_=flat)
-            hidden(
-                t,
-                [c[:, slot(t, z) * P : (slot(t, z) + 1) * P] for z in range(PASSES)],
-                [s[:, slot(t, z) * P : (slot(t, z) + 1) * P] for z in range(PASSES)],
-                banks,
-                False,
+        def quantize_w1(t, z):
+            codes[t, z] = sb([P, P], U32, f"w1_codes{t}_{z}")
+            scales[t, z] = sb([P, P], U8, f"w1_scales{t}_{z}")
+            nc.vector.quantize_mx(
+                out=codes[t, z][:].bitcast(FP8X4),
+                scales=scales[t, z][:],
+                in_=grouped[t, z][:].rearrange("p c j -> p (c j)"),
             )
 
-        def add_turned(dst, values, start=False, stop=False):
-            nc.tensor.matmul(out=dst, lhsT=values, rhs=ident[:], is_transpose=True, start=start, stop=stop)
+        def cast_half(t, z, tag="", copy=nc.scalar.copy):
+            if z == 0:
+                grouped[t] = sb([P, PASSES * P * PACK], BF16, f"w1_grouped{t}", tag)
+            room = grouped[t][:, z * P * PACK : (z + 1) * P * PACK].rearrange("p (c j) -> p c j", j=PACK)
+            dst, src = interleave_views(room, w1_raw[t, z])
+            copy(out=dst, in_=src)
 
-        def own_value(t, b0, b1, acc, start, stop=False):
+        def quantize_both(t):
+            c = sb([P, PASSES * P], U32, f"w1_codes{t}")
+            s = sb([P, PASSES * P], U8, f"w1_scales{t}")
+            nc.vector.quantize_mx(out=c[:].bitcast(FP8X4), scales=s[:], in_=grouped[t][:])
+            for z in range(PASSES):
+                codes[t, z] = c[:, z * P : (z + 1) * P]
+                scales[t, z] = s[:, z * P : (z + 1) * P]
+
+        h_bank = {B: 0, C: 4, E: 3}
+
+        def product(t, z, c0, c1, k):
+            if z == 0:
+                accs[t, c0] = bank(k, [P, c1 - c0], f"h_acc{t}_{c0}")
+            nc.tensor.matmul_mx(
+                out=accs[t, c0][:],
+                lhsT=codes[t, z][:].bitcast(FP8X4),
+                lhsT_scale=scales[t, z][:],
+                rhs=x_codes[z][:, c0:c1].bitcast(FP8X4),
+                rhs_scale=x_planes[:, z, c0:c1],
+                start=(z == 0),
+                stop=(z == PASSES - 1),
+            )
+
+        def both_passes(t):
+            quantize_both(t)
+            for z in range(PASSES):
+                product(t, z, 0, T, h_bank[t])
+
+        def gelu(t, c0, c1):
+            nc.scalar.activation(out=h[t][:, c0:c1], in_=accs[t, c0][:], func=GELU)
+
+        def turn(sums, values, b0, b1, start=False, stop=False):
             for b in range(b0, b1):
-                add_turned(
-                    acc[:, b - b0, :], h[t][:, b * P : (b + 1) * P], start=start and b == b0, stop=stop and b == b1 - 1
+                nc.tensor.matmul(
+                    out=sums[b][0],
+                    lhsT=values[:, (b - b0) * P : (b - b0 + 1) * P],
+                    rhs=ident[:],
+                    is_transpose=True,
+                    start=start and sums[b][1],
+                    stop=stop and sums[b][2],
                 )
 
-        def neighbour(t, d, b0, b1, acc, stop, acc_high=None, start=False):
-            width = (b1 - b0) * P
-            term = places[t, d, b0] if (t, d, b0) in places else sb([P, width], F32, f"term{t}_{d}_{b0}")[:]
+        def open_sums(t, groups):
+            sums = {}
+            for b0, b1, k in groups:
+                acc = bank(k, [P, b1 - b0, P], f"sum{t}_{b0}")
+                for b in range(b0, b1):
+                    sums[b] = (acc[:, b - b0, :], b == b0, b == b1 - 1, acc)
+            return sums
+
+        def gather_gated(t, d, b0, b1, term=None):
+            if term is None:
+                term = sb([P, (b1 - b0) * P], F32, f"term{t}_{d}_{b0}")[:]
             nc.vector.tensor_tensor(
                 term,
                 h[t][:].indirect(offsets[d][:, b0 * P // 16 : b1 * P // 16]),
                 minus_gate[d][:, b0 * P : b1 * P],
                 MULT,
             )
-            for b in range(b0, b1):
-                dst = acc_high[b] if acc_high and b in acc_high else acc[:, b - b0, :]
-                add_turned(
-                    dst,
-                    term[:, (b - b0) * P : (b - b0 + 1) * P],
-                    start=start and b == b0,
-                    stop=stop and (b == b1 - 1 or t == E),
-                )
+            return term
 
-        pieces = [(0, 2), (2, 3), (3, 4)]
-        z_words = {}
+        def gather_plain(t, d, fetched):
+            nc.scalar.activation(out=fetched, in_=h[t][:].indirect(offsets[d][:]), func=COPY)
+            return fetched
 
-        def round_z(t, b0, b1, acc, first=None):
-            first = b0 if first is None else first
-            src = acc.rearrange("v b (p u e) -> v b u p e", u=2, e=2)
-            rows = z_words[first].bitcast(BF16).rearrange("v (b u p e) -> v b u p e", u=2, p=P, e=2)
-            nc.scalar.copy(out=rows[:, b0 - first : b1 - first, :, 32 * t : 32 * (t + 1), :], in_=src)
+        def apply_gate(t, d, fetched, b0, b1, term=None):
+            if term is None:
+                term = sb([P, (b1 - b0) * P], F32, f"term{t}_{d}_{b0}")[:]
+            nc.vector.tensor_tensor(term, fetched[:, b0 * P : b1 * P], minus_gate[d][:, b0 * P : b1 * P], MULT)
+            return term
 
-        def round_all(t, first, acc):
-            for b0, b1 in pieces:
-                if b0 >= first:
-                    round_z(t, b0, b1, acc[:, b0 - first : b1 - first, :])
+        def round_z(t, b0, b1, acc, copy=nc.scalar.copy):
+            src = acc[:].rearrange("v b (p u e) -> v b u p e", u=2, e=2)
+            rows = z_words.bitcast(BF16).rearrange("v (b u p e) -> v b u p e", u=2, p=P, e=2)
+            copy(out=rows[:, b0:b1, :, 32 * t : 32 * (t + 1), :], in_=src)
 
         out_rows = out.rearrange("(a m) v -> m a v", a=M_TILES)
         z_grouped = {}
@@ -236,9 +222,8 @@ def tile_picked_wlapl_gelu_l_kernel(
             back = bank(k, [P, n, 2, P], f"back{b0}")
             for b in range(n):
                 for u in range(2):
-                    nc.tensor.transpose(
-                        back[:, b, u, :], z_words[b0][:, (2 * b + u) * P : (2 * b + u + 1) * P], ident[:]
-                    )
+                    w0 = (2 * (b0 + b) + u) * P
+                    nc.tensor.transpose(back[:, b, u, :], z_words[:, w0 : w0 + P], ident[:])
             z_grouped[b0] = sb([P, n * 2 * P], F32, f"z_grouped{b0}")[:]
             nc.scalar.copy(
                 out=z_grouped[b0].rearrange("p (b v u) -> p b v u", b=n, u=2),
@@ -247,10 +232,10 @@ def tile_picked_wlapl_gelu_l_kernel(
 
         def quantize_z(b0, b1):
             width = (b1 - b0) * P
-            codes = sb([P, width], U32, f"z_codes{b0}")
-            scales = sb([P, width], U8, f"z_scales{b0}")
-            nc.vector.quantize_mx(out=codes[:].bitcast(FP8X4), scales=scales[:], in_=z_grouped[b0].bitcast(BF16))
-            return codes, scales
+            zc = sb([P, width], U32, f"z_codes{b0}")
+            zs = sb([P, width], U8, f"z_scales{b0}")
+            nc.vector.quantize_mx(out=zc[:].bitcast(FP8X4), scales=zs[:], in_=z_grouped[b0].bitcast(BF16))
+            return zc, zs
 
         def project(dst, a, z_mx):
             nc.tensor.matmul_mx(
@@ -263,79 +248,91 @@ def tile_picked_wlapl_gelu_l_kernel(
                 stop=True,
             )
 
-        early_hidden(A, nc.vector.tensor_copy, ("", ""), (0, 1))
-        early_hidden(B, nc.scalar.copy, (f"w1_codes{A}_1", f"w1_scales{A}_1"), (3, 4))
-        sum_a = bank(5, [P, 4, P], "sum_a")
-        own_value(A, 0, 4, sum_a, True)
-        neighbour(A, 0, 0, 4, sum_a, False)
-        neighbour(A, 1, 0, 2, sum_a, False)
-        neighbour(A, 1, 2, 4, sum_a[:, 2:], False)
-        neighbour(A, 2, 0, 4, sum_a, True)
-        grouped_c = cast_w1(C)
-        grouped_e = cast_w1(E, f"w1_scales{B}_1")
-        sum_b = bank(2, [P, 4, P], "sum_b")
-        neighbour(B, 0, 0, 4, sum_b, False, start=True)
-        later_hidden(C, grouped_c, (0, 1))
-        neighbour(B, 1, 0, 4, sum_b, False)
-        later_hidden(E, grouped_e, (3, 4))
-        neighbour(B, 2, 0, 4, sum_b, False)
-        own_value(B, 0, 4, sum_b, False, True)
+        for z in range(PASSES):
+            cast_w1(A, z, nc.vector.tensor_copy)
+            quantize_w1(A, z)
+        for z in range(PASSES):
+            for i in range(2):
+                product(A, z, i * half, (i + 1) * half, i)
+        for i in range(2):
+            gelu(A, i * half, (i + 1) * half)
+        cast_half(B, 0, f"w1_scales{A}_1", nc.vector.tensor_copy)
+        sum_bank = {A: 5, B: 2, C: 6}
+        sums, w2_grouped = {}, {}
 
-        w2_grouped = sb([P, N * PACK], BF16, "w2_grouped", f"w1_codes{E}")[:]
-        for (b0, b1), tag in zip(pieces, (f"w1_scales{B}_1", f"w1_scales{C}", "w1_raw_ce0")):
-            z_words[b0] = sb([P, (b1 - b0) * 2 * P], F32, f"z_words{b0}", tag)[:]
-        round_all(A, 0, sum_a[:])
-        round_all(B, 0, sum_b[:])
-        dst, src = interleave_views(w2_grouped.rearrange("p (n j) -> p n j", j=PACK), w2_raw)
-        nc.scalar.copy(out=dst, in_=src)
+        w2_tags = (f"w1_codes{E}", f"w1_scales{E}")
 
-        sum_c01 = bank(0, [P, 2, P], "sum_c01")
-        sum_e0 = bank(2, [P, 1, P], "sum_e0")
-        sum_e1 = bank(6, [P, 1, P], "sum_e1")
-        sum_c23 = bank(1, [P, 2, P], "sum_c23")
-        own_value(C, 0, 2, sum_c01, True)
-        own_value(C, 2, 4, sum_c23, True)
-        for d in range(2):
-            neighbour(C, d, 0, 4, sum_c01, False, {2: sum_c23[:, 0, :], 3: sum_c23[:, 1, :]})
-        neighbour(C, 2, 0, 2, sum_c01, True)
-        round_z(C, 0, 2, sum_c01[:])
-        own_value(E, 0, 1, sum_e0, True)
-        own_value(E, 1, 2, sum_e1, True)
-        for d in range(D):
-            neighbour(E, d, 0, 2, sum_e0, d == D - 1, {1: sum_e1[:, 0, :]})
-        round_z(E, 0, 1, sum_e0[:])
-        round_z(E, 1, 2, sum_e1[:], 0)
-        turn_back(0, 2, 3)
-        sum_e2 = bank(2, [P, 1, P], "sum_e2")
-        sum_e3 = bank(6, [P, 1, P], "sum_e3")
-        own_value(E, 2, 3, sum_e2, True)
-        own_value(E, 3, 4, sum_e3, True)
-        neighbour(C, 2, 2, 4, sum_c23, True)
-        round_all(C, 2, sum_c23[:])
-        neighbour(E, 0, 2, 4, sum_e2, False, {3: sum_e3[:, 0, :]})
-        for d in (1, 2):
-            neighbour(E, d, 2, 3, sum_e2, d == D - 1)
-        round_z(E, 2, 3, sum_e2[:])
-        for d in (1, 2):
-            neighbour(E, d, 3, 4, sum_e3, d == D - 1)
-        round_z(E, 3, 4, sum_e3[:])
-        turn_back(2, 3, 4)
-        turn_back(3, 4, 5)
+        def cast_w2(a):
+            w2_grouped[a] = sb([P, P, PACK], BF16, f"w2_grouped{a}", w2_tags[a])[:]
+            dst, src = interleave_views(w2_grouped[a], w2_raw[:, :, a * P : (a + 1) * P])
+            nc.scalar.copy(out=dst, in_=src)
 
-        w2_codes = sb([P, N], U32, "w2_codes")
+        cast_half(B, 1)
+        for t in (A, B, C):
+            sums[t] = open_sums(t, [(0, 4, sum_bank[t])])
+            turn(sums[t], h[t], 0, 4, start=True)
+            if t == A:
+                term = gather_gated(A, 0, 0, 2)
+                both_passes(B)
+                turn(sums[A], term, 0, 2)
+                turn(sums[A], gather_gated(A, 0, 2, 4, strip[:, T : T + half]), 2, 4)
+            else:
+                turn(sums[t], gather_gated(t, 0, 0, 4, rooms[C] if t == B else None), 0, 4)
+            fetched = gather_plain(t, 2, strip[:, T + half :] if t == A else sb([P, T], F32, f"fetched{t}")[:])
+            turn(sums[t], gather_gated(t, 1, 0, 4, strip[:, :T] if t == A else None), 0, 4)
+            if t < C:
+                cast_half(t + 2, 0, f"w1_codes{A}_1" if t == A else f"w1_codes{B}")
+                cast_half(t + 2, 1)
+            if t == B:
+                z_words = sb([P, 4 * 2 * P], F32, "z_words", "w1_raw_e0")[:]
+                round_z(A, 0, 4, sums[A][0][3])
+            gelu(t + 1, 0, T)
+            if t == B:
+                both_passes(E)
+            turn(sums[t], apply_gate(t, 2, fetched, 0, 4, rooms[E] if t == B else None), 0, 4, stop=True)
+            if t == A:
+                both_passes(C)
+
+        sums[E] = open_sums(E, [(0, 2, 1), (2, 3, 7), (3, 4, 0)])
+        cast_w2(0)
+        fetched = gather_plain(E, 2, sb([P, T], F32, "fetched_e")[:])
+        cast_w2(1)
+        round_z(B, 0, 4, sums[B][0][3])
+        round_z(C, 0, 4, sums[C][0][3])
+        turn(sums[E], h[E], 0, 4, start=True)
+        turn(sums[E], gather_gated(E, 0, 0, 2), 0, 2)
+        turn(sums[E], gather_gated(E, 1, 0, 2), 0, 2)
+        turn(sums[E], apply_gate(E, 2, fetched, 0, 2), 0, 2, stop=True)
+        round_z(E, 0, 2, sums[E][0][3])
+        turn_back(0, 2, 5)
+        turn(sums[E], apply_gate(E, 2, fetched, 2, 4), 2, 4)
+        turn(sums[E], gather_gated(E, 0, 2, 4, fetched[:, :half]), 2, 4)
+        w2_codes = sb([P, N], U32, "w2_codes", f"term{E}_2_0")
         w2_scales = sb([P, N], U8, "w2_scales")
-        nc.vector.quantize_mx(out=w2_codes[:].bitcast(FP8X4), scales=w2_scales[:], in_=w2_grouped)
+        for a in range(M_TILES):
+            nc.vector.quantize_mx(
+                out=w2_codes[:, a * P : (a + 1) * P].bitcast(FP8X4),
+                scales=w2_scales[:, a * P : (a + 1) * P],
+                in_=w2_grouped[a].rearrange("p n j -> p (n j)"),
+            )
+        for b in (2, 3):
+            last = gather_gated(E, 1, b, b + 1, sb([P, P], F32, f"last{b}", w2_tags[b - 2])[:])
+            turn(sums[E], last, b, b + 1, stop=True)
+            round_z(E, b, b + 1, sums[E][b][3], nc.vector.tensor_copy)
+        turn_back(2, 3, 4)
+        turn_back(3, 4, 2)
+
         z01 = quantize_z(0, 2)
         z2 = quantize_z(2, 3)
         z3 = quantize_z(3, 4)
 
-        out_01 = [bank(k, [P, 2 * P], f"out_01{k}") for k in (6, 5)]
+        out_01 = [bank(k, [P, 2 * P], f"out_01{k}") for k in (3, 6)]
         for a in range(M_TILES):
             project(out_01[a][:], a, z01)
-        out_2 = bank(2, [P, M_TILES, P], "out_2")
+        out_2 = bank(1, [P, M_TILES, P], "out_2")
         for a in range(M_TILES):
             project(out_2[:, a, :], a, z2)
-        out_3 = [bank(a, [P, P], f"out_3{a}") for a in range(M_TILES)]
+        out_3 = [bank(k, [P, P], f"out_3{k}") for k in (7, 0)]
         for a in range(M_TILES):
             project(out_3[a][:], a, z3)
 

from contextlib import ExitStack

import concourse.mybir as mybir
from concourse.masks import make_identity

K, T, D, H, N = 1024, 512, 3, 512, 256
FLOPS = 2 * K * H * T + 2 * H * N * T

F32 = mybir.dt.float32
BF16 = mybir.dt.bfloat16
I32 = mybir.dt.int32
U32 = mybir.dt.uint32
U16 = mybir.dt.uint16
U8 = mybir.dt.uint8
FP8X4 = mybir.dt.float8_e4m3fn_x4
GELU = mybir.ActivationFunctionType.Gelu_apprx_tanh
COPY = mybir.ActivationFunctionType.Copy
MULT = mybir.AluOpType.mult

P = 128
PACK = 4
PASSES = K // (P * PACK)
M_TILES = N // P
SPARE = 16
ALIGN = 64
A, B, C, E = 0, 1, 2, 3


def interleave_views(grouped, raw):
    return (
        grouped.rearrange("p (c i) j -> p c j i", i=4),
        raw.rearrange("p j (c i) -> p c j i", i=4),
    )


def tile_picked_wlapl_gelu_l_kernel(
    tc, x_words, x_scales, w1, w2, gate, pos1, pos2, pos3, out
):
    nc = tc.nc
    with ExitStack() as ctx:
        lists = ctx.enter_context(tc.tile_pool(name="lists", bufs=1))
        keep = ctx.enter_context(tc.tile_pool(name="keep", bufs=1))
        psum = ctx.enter_context(tc.psum_pool(name="psum", bufs=1))

        def sb(shape, dtype, name, tag=""):
            return keep.tile(shape, dtype, name=name, tag=tag or name, align_bytes=ALIGN)

        def bank(k, shape, name):
            return psum.tile(shape, F32, name=name, tag=f"bank{k}")

        x_planes = sb([P, PASSES, T], U8, "x_planes")
        nc.gpsimd.memset(x_planes[:].rearrange("p z c -> p (z c)").bitcast(I32), 0)
        zeros = sb([P, SPARE], F32, "zeros")
        nc.vector.memset(zeros[:], 0.0)
        h = [sb([P, T + SPARE], F32, f"h{t}") for t in range(4)]
        nc.scalar.activation(out=h[A][:, T:], in_=zeros[:], func=GELU)
        ident = sb([P, P], F32, "ident")
        make_identity(nc, ident[:])
        for t in (B, C, E):
            nc.gpsimd.memset(h[t][:, T:], 0.0)

        w1_rows = w1.rearrange("(z p j) c -> z p j c", z=PASSES, j=PACK)
        w1_raw = {}
        half = T // 2

        def load_w1(t, z, room):
            w1_raw[t, z] = room.rearrange("p (j c) -> p j c", j=PACK)
            nc.sync.dma_start(out=w1_raw[t, z], in_=w1_rows[z, :, :, t * P : (t + 1) * P])

        strip = sb([P, 2 * T + half], F32, "strip")
        rooms = {t: sb([P, T], F32, f"room{t}")[:] for t in (C, E)}

        gate_cols = sb([P, D, 8], F32, "gate_cols")
        nc.sync.dma_start(out=gate_cols[:, :, :PACK], in_=gate[:, 0, :].rearrange("d (p b) -> p d b", b=PACK))
        load_w1(A, 0, sb([P, T], F32, "w1_raw_a0")[:])
        scale_rows = x_scales.rearrange("z (q r) c -> r q z c", r=4)
        for r in range(4):
            nc.sync.dma_start(out=x_planes[r:P:32].bitcast(I32), in_=scale_rows[r].bitcast(I32))
        load_w1(A, 1, sb([P, T], F32, "w1_raw_a1")[:])
        x_codes = [sb([P, T], U32, f"x_codes{z}") for z in range(PASSES)]

        def load_x(z, c0, c1):
            nc.sync.dma_start(
                out=x_codes[z][:, c0:c1].bitcast(I32),
                in_=x_words[z, :, c0:c1, :].rearrange("p n r -> p (n r)").bitcast(I32),
            )

        load_x(0, 0, T)
        load_x(1, 0, half)
        load_x(1, half, T)
        offsets = [lists.tile([P, T // 16], U16, name=f"offsets{d}") for d in range(D)]
        nc.sync.dma_start(offsets[0][:], pos1)
        load_w1(B, 0, sb([P, T], F32, "w1_raw_b0")[:])
        load_w1(B, 1, strip[:, T - P : 2 * T - P])
        nc.sync.dma_start(offsets[2][:], pos3)
        nc.sync.dma_start(offsets[1][:], pos2)
        load_w1(C, 0, sb([P, T], F32, "w1_raw_c0")[:])
        load_w1(C, 1, rooms[C])
        load_w1(E, 0, sb([P, T], F32, "w1_raw_e0")[:])
        load_w1(E, 1, rooms[E])
        w2_raw = sb([P, PACK, N], F32, "w2_raw")[:]
        nc.sync.dma_start(out=w2_raw, in_=w2.rearrange("(p j) n -> p j n", j=PACK))

        minus_gate = []
        for d in range(D):
            spread = bank(d, [P, PACK, P], f"spread{d}")
            for b in range(PACK):
                nc.tensor.transpose(spread[:, b, :], gate_cols[:, d, b : b + 1].to_broadcast([P, P]), ident[:])
            g = sb([P, T], F32, f"minus_gate{d}")
            nc.scalar.activation(
                out=g[:].rearrange("p (n b) -> p n b", b=PACK),
                in_=spread[:].rearrange("p b n -> p n b"),
                func=COPY,
                scale=-1.0,
            )
            minus_gate.append(g)

        grouped, codes, scales, accs = {}, {}, {}, {}

        def cast_w1(t, z, copy, tag=""):
            grouped[t, z] = sb([P, P, PACK], BF16, f"w1_grouped{t}_{z}", tag)
            dst, src = interleave_views(grouped[t, z][:], w1_raw[t, z])
            copy(out=dst, in_=src)

        def quantize_w1(t, z):
            codes[t, z] = sb([P, P], U32, f"w1_codes{t}_{z}")
            scales[t, z] = sb([P, P], U8, f"w1_scales{t}_{z}")
            nc.vector.quantize_mx(
                out=codes[t, z][:].bitcast(FP8X4),
                scales=scales[t, z][:],
                in_=grouped[t, z][:].rearrange("p c j -> p (c j)"),
            )

        def cast_half(t, z, tag="", copy=nc.scalar.copy):
            if z == 0:
                grouped[t] = sb([P, PASSES * P * PACK], BF16, f"w1_grouped{t}", tag)
            room = grouped[t][:, z * P * PACK : (z + 1) * P * PACK].rearrange("p (c j) -> p c j", j=PACK)
            dst, src = interleave_views(room, w1_raw[t, z])
            copy(out=dst, in_=src)

        def quantize_both(t):
            c = sb([P, PASSES * P], U32, f"w1_codes{t}")
            s = sb([P, PASSES * P], U8, f"w1_scales{t}")
            nc.vector.quantize_mx(out=c[:].bitcast(FP8X4), scales=s[:], in_=grouped[t][:])
            for z in range(PASSES):
                codes[t, z] = c[:, z * P : (z + 1) * P]
                scales[t, z] = s[:, z * P : (z + 1) * P]

        h_bank = {B: 0, C: 4, E: 3}

        def product(t, z, c0, c1, k):
            if z == 0:
                accs[t, c0] = bank(k, [P, c1 - c0], f"h_acc{t}_{c0}")
            nc.tensor.matmul_mx(
                out=accs[t, c0][:],
                lhsT=codes[t, z][:].bitcast(FP8X4),
                lhsT_scale=scales[t, z][:],
                rhs=x_codes[z][:, c0:c1].bitcast(FP8X4),
                rhs_scale=x_planes[:, z, c0:c1],
                start=(z == 0),
                stop=(z == PASSES - 1),
            )

        def both_passes(t):
            quantize_both(t)
            for z in range(PASSES):
                product(t, z, 0, T, h_bank[t])

        def gelu(t, c0, c1):
            nc.scalar.activation(out=h[t][:, c0:c1], in_=accs[t, c0][:], func=GELU)

        def turn(sums, values, b0, b1, start=False, stop=False):
            for b in range(b0, b1):
                nc.tensor.matmul(
                    out=sums[b][0],
                    lhsT=values[:, (b - b0) * P : (b - b0 + 1) * P],
                    rhs=ident[:],
                    is_transpose=True,
                    start=start and sums[b][1],
                    stop=stop and sums[b][2],
                )

        def open_sums(t, groups):
            sums = {}
            for b0, b1, k in groups:
                acc = bank(k, [P, b1 - b0, P], f"sum{t}_{b0}")
                for b in range(b0, b1):
                    sums[b] = (acc[:, b - b0, :], b == b0, b == b1 - 1, acc)
            return sums

        def gather_gated(t, d, b0, b1, term=None):
            if term is None:
                term = sb([P, (b1 - b0) * P], F32, f"term{t}_{d}_{b0}")[:]
            nc.vector.tensor_tensor(
                term,
                h[t][:].indirect(offsets[d][:, b0 * P // 16 : b1 * P // 16]),
                minus_gate[d][:, b0 * P : b1 * P],
                MULT,
            )
            return term

        def gather_plain(t, d, fetched):
            nc.scalar.activation(out=fetched, in_=h[t][:].indirect(offsets[d][:]), func=COPY)
            return fetched

        def apply_gate(t, d, fetched, b0, b1, term=None):
            if term is None:
                term = sb([P, (b1 - b0) * P], F32, f"term{t}_{d}_{b0}")[:]
            nc.vector.tensor_tensor(term, fetched[:, b0 * P : b1 * P], minus_gate[d][:, b0 * P : b1 * P], MULT)
            return term

        def round_z(t, b0, b1, acc, copy=nc.scalar.copy):
            src = acc[:].rearrange("v b (p u e) -> v b u p e", u=2, e=2)
            rows = z_words.bitcast(BF16).rearrange("v (b u p e) -> v b u p e", u=2, p=P, e=2)
            copy(out=rows[:, b0:b1, :, 32 * t : 32 * (t + 1), :], in_=src)

        out_rows = out.rearrange("(a m) v -> m a v", a=M_TILES)
        z_grouped = {}

        def turn_back(b0, b1, k):
            n = b1 - b0
            back = bank(k, [P, n, 2, P], f"back{b0}")
            for b in range(n):
                for u in range(2):
                    w0 = (2 * (b0 + b) + u) * P
                    nc.tensor.transpose(back[:, b, u, :], z_words[:, w0 : w0 + P], ident[:])
            z_grouped[b0] = sb([P, n * 2 * P], F32, f"z_grouped{b0}")[:]
            nc.scalar.copy(
                out=z_grouped[b0].rearrange("p (b v u) -> p b v u", b=n, u=2),
                in_=back[:].rearrange("p b u v -> p b v u"),
            )

        def quantize_z(b0, b1):
            width = (b1 - b0) * P
            zc = sb([P, width], U32, f"z_codes{b0}")
            zs = sb([P, width], U8, f"z_scales{b0}")
            nc.vector.quantize_mx(out=zc[:].bitcast(FP8X4), scales=zs[:], in_=z_grouped[b0].bitcast(BF16))
            return zc, zs

        def project(dst, a, z_mx):
            nc.tensor.matmul_mx(
                out=dst,
                lhsT=w2_codes[:, a * P : (a + 1) * P].bitcast(FP8X4),
                lhsT_scale=w2_scales[:, a * P : (a + 1) * P],
                rhs=z_mx[0][:].bitcast(FP8X4),
                rhs_scale=z_mx[1][:],
                start=True,
                stop=True,
            )

        for z in range(PASSES):
            cast_w1(A, z, nc.vector.tensor_copy)
            quantize_w1(A, z)
        for z in range(PASSES):
            for i in range(2):
                product(A, z, i * half, (i + 1) * half, i)
        for i in range(2):
            gelu(A, i * half, (i + 1) * half)
        cast_half(B, 0, f"w1_scales{A}_1", nc.vector.tensor_copy)
        sum_bank = {A: 5, B: 2, C: 6}
        sums, w2_grouped = {}, {}

        w2_tags = (f"w1_codes{E}", f"w1_scales{E}")

        def cast_w2(a):
            w2_grouped[a] = sb([P, P, PACK], BF16, f"w2_grouped{a}", w2_tags[a])[:]
            dst, src = interleave_views(w2_grouped[a], w2_raw[:, :, a * P : (a + 1) * P])
            nc.scalar.copy(out=dst, in_=src)

        cast_half(B, 1)
        for t in (A, B, C):
            sums[t] = open_sums(t, [(0, 4, sum_bank[t])])
            turn(sums[t], h[t], 0, 4, start=True)
            if t == A:
                term = gather_gated(A, 0, 0, 2)
                both_passes(B)
                turn(sums[A], term, 0, 2)
                turn(sums[A], gather_gated(A, 0, 2, 4, strip[:, T : T + half]), 2, 4)
            else:
                turn(sums[t], gather_gated(t, 0, 0, 4, rooms[C] if t == B else None), 0, 4)
            fetched = gather_plain(t, 2, strip[:, T + half :] if t == A else sb([P, T], F32, f"fetched{t}")[:])
            turn(sums[t], gather_gated(t, 1, 0, 4, strip[:, :T] if t == A else None), 0, 4)
            if t < C:
                cast_half(t + 2, 0, f"w1_codes{A}_1" if t == A else f"w1_codes{B}")
                cast_half(t + 2, 1)
            if t == B:
                z_words = sb([P, 4 * 2 * P], F32, "z_words", "w1_raw_e0")[:]
                round_z(A, 0, 4, sums[A][0][3])
            gelu(t + 1, 0, T)
            if t == B:
                both_passes(E)
            turn(sums[t], apply_gate(t, 2, fetched, 0, 4, rooms[E] if t == B else None), 0, 4, stop=True)
            if t == A:
                both_passes(C)

        sums[E] = open_sums(E, [(0, 2, 1), (2, 3, 7), (3, 4, 0)])
        cast_w2(0)
        fetched = gather_plain(E, 2, sb([P, T], F32, "fetched_e")[:])
        cast_w2(1)
        round_z(B, 0, 4, sums[B][0][3])
        round_z(C, 0, 4, sums[C][0][3])
        turn(sums[E], h[E], 0, 4, start=True)
        turn(sums[E], gather_gated(E, 0, 0, 2), 0, 2)
        turn(sums[E], gather_gated(E, 1, 0, 2), 0, 2)
        turn(sums[E], apply_gate(E, 2, fetched, 0, 2), 0, 2, stop=True)
        round_z(E, 0, 2, sums[E][0][3])
        turn_back(0, 2, 5)
        turn(sums[E], apply_gate(E, 2, fetched, 2, 4), 2, 4)
        turn(sums[E], gather_gated(E, 0, 2, 4, fetched[:, :half]), 2, 4)
        w2_codes = sb([P, N], U32, "w2_codes", f"term{E}_2_0")
        w2_scales = sb([P, N], U8, "w2_scales")
        for a in range(M_TILES):
            nc.vector.quantize_mx(
                out=w2_codes[:, a * P : (a + 1) * P].bitcast(FP8X4),
                scales=w2_scales[:, a * P : (a + 1) * P],
                in_=w2_grouped[a].rearrange("p n j -> p (n j)"),
            )
        for b in (2, 3):
            last = gather_gated(E, 1, b, b + 1, sb([P, P], F32, f"last{b}", w2_tags[b - 2])[:])
            turn(sums[E], last, b, b + 1, stop=True)
            round_z(E, b, b + 1, sums[E][b][3], nc.vector.tensor_copy)
        turn_back(2, 3, 4)
        turn_back(3, 4, 2)

        z01 = quantize_z(0, 2)
        z2 = quantize_z(2, 3)
        z3 = quantize_z(3, 4)

        out_01 = [bank(k, [P, 2 * P], f"out_01{k}") for k in (3, 6)]
        for a in range(M_TILES):
            project(out_01[a][:], a, z01)
        out_2 = bank(1, [P, M_TILES, P], "out_2")
        for a in range(M_TILES):
            project(out_2[:, a, :], a, z2)
        out_3 = [bank(k, [P, P], f"out_3{k}") for k in (7, 0)]
        for a in range(M_TILES):
            project(out_3[a][:], a, z3)

        for a in range(M_TILES):
            result_01 = sb([P, 2 * P], F32, f"result_01{a}")
            if a == 0:
                nc.scalar.copy(out=result_01[:], in_=out_01[a][:])
            else:
                nc.vector.tensor_copy(out=result_01[:], in_=out_01[a][:])
            nc.sync.dma_start(out=out_rows[:, a, : 2 * P], in_=result_01[:])
        result_2 = sb([P, M_TILES, P], F32, "result_2")
        nc.scalar.copy(out=result_2[:], in_=out_2[:])
        nc.sync.dma_start(out=out_rows[:, :, 2 * P : 3 * P], in_=result_2[:])
        low = sb([P, P], F32, "result_low")
        high = sb([P, P], F32, "result_high")
        nc.vector.tensor_copy(out=low[:], in_=out_3[0][:])
        nc.sync.dma_start(out=out_rows[:, 0, 3 * P :], in_=low[:])
        nc.scalar.copy(out=high[:], in_=out_3[1][:])
        nc.scalar.dma_start(out=out_rows[:, 1, 3 * P :], in_=high[:])
